import numpy as np
import ml_dtypes


def mxq(x, axis, fmt="e4m3"):
    dtype, down = {"e4m3": (ml_dtypes.float8_e4m3fn, 7), "e5m2": (ml_dtypes.float8_e5m2, 14)}[fmt]
    v = np.moveaxis(np.asarray(x, np.float32).astype(ml_dtypes.bfloat16).astype(np.float64), axis, -1)
    blocks = v.reshape(v.shape[:-1] + (-1, 32))
    amax = np.abs(blocks).max(-1, keepdims=True)
    byte = np.maximum(np.where(amax > 0, np.frexp(amax)[1] - 1 + 127, 0) - down, 1)
    scale = np.exp2(byte - 127.0)
    codes = (blocks / scale).astype(np.float32).astype(dtype).astype(np.float64)
    return np.moveaxis((codes * scale).reshape(v.shape), -1, axis)


WIDE = False


def mx_kscale(k):
    if not WIDE:
        return np.ones(k)
    levels = np.array([10, -10, 5, -5, 0])
    if k % 512:
        return np.exp2(np.random.permutation(np.resize(levels, k // 32))).repeat(32)
    a = np.empty((k // 512, 16))
    for p in range(k // 512):
        a[p, :8] = np.random.permutation(np.resize(levels, 8))
        for g in range(8):
            far = levels[np.abs(levels - a[p, g]) >= 10]
            a[p, g + 8] = far[np.random.randint(len(far))]
    return np.exp2(a.ravel()).repeat(32)


def f64(x):
    return np.asarray(x).astype(np.float64)


def striped(idx):
    return np.tile(idx.reshape(-1, 16).T, (8, 1)).astype(np.uint16)


def unstriped(offs):
    return offs[:16].T.reshape(-1).astype(np.int64)


def pack_weight(w):
    k, n = w.shape
    w = f64(np.asarray(w, np.float32).astype(ml_dtypes.bfloat16)).reshape(k // 32, 32, n)
    amax = np.abs(w).max(1)
    byte = np.clip(np.where(amax > 0, np.frexp(amax)[1] - 1 + 127 - 7, 1), 1, 254)
    scaled = (w * np.exp2(127.0 - byte)[:, None, :]).reshape(k, n).astype(np.float32)
    words = np.ascontiguousarray(scaled.reshape(k // 512, 128, 4, n).transpose(0, 1, 3, 2)).astype(ml_dtypes.float8_e4m3fn).view(np.uint8)
    return words, np.ascontiguousarray(byte.astype(np.uint8).reshape(k // 512, 16, n))


def unpack_weight(words, scales):
    g, p, n, _ = words.shape
    vals = np.ascontiguousarray(words).view(ml_dtypes.float8_e4m3fn).astype(np.float64) * np.repeat(np.exp2(scales.astype(np.float64) - 127.0), 8, axis=1)[..., None]
    return vals.transpose(0, 1, 3, 2).reshape(g * 512, n)


def relu(v):
    return np.maximum(v, 0.0)


K, T, S, D, V, H, N, U = 1024, 2048, 512, 2, 512, 512, 128, 1024
P = 2 ** 7


def setup_inputs():
    n = np.random.standard_normal
    s = mx_kscale(K)[:, None]
    u = mx_kscale(H)
    packed_xT = pack_weight(n((K, T)) * s)
    packed_w2 = pack_weight(n((H, N)) / np.sqrt(H) / u[:, None])
    return {
        "x_words": packed_xT[0],
        "x_scales": packed_xT[1],
        "w1": (n((K, H)) / np.sqrt(K) / s * u).astype(np.float32),
        "w2_words": packed_w2[0],
        "w2_scales": packed_w2[1],
        "gate": np.tile(np.random.uniform(0.2, 0.6, (D, 1, V)), (1, P, 1)).astype(np.float32),
        "emb": (0.5 * n((H, U)) * u[:, None]).astype(np.float32),
        "offs": striped(np.random.permutation(T)[:S]),
        "cell": striped(np.random.permutation(U)[:S]),
        "pos1": striped(np.random.permutation(U)[:V]),
        "pos2": striped(np.random.permutation(U)[:V]),
    }


def reference(x_words, x_scales, w1, w2_words, w2_scales, gate, emb, offs, cell, pos1, pos2):
    xq = unpack_weight(x_words, x_scales)[:, unstriped(offs)]
    up = np.zeros((H, U))
    up[:, unstriped(cell)] = relu(mxq(f64(w1), 0, "e4m3").T @ xq)
    z = up + f64(emb)
    y = unpack_weight(w2_words, w2_scales).T @ mxq(z, 0, "e4m3")
    return y[:, unstriped(pos1)] * f64(gate)[0, :1] + y[:, unstriped(pos2)] * f64(gate)[1, :1]

@@ -1,0 +1,256 @@
+from contextlib import ExitStack
+
+import concourse.mybir as mybir
+from concourse.masks import make_identity
+
+K, T, S, V, H, N, U = 1024, 2048, 512, 512, 512, 128, 1024
+FLOPS = 2 * K * H * S + 2 * H * N * U
+
+F32 = mybir.dt.float32
+BF16 = mybir.dt.bfloat16
+I32 = mybir.dt.int32
+U32 = mybir.dt.uint32
+U16 = mybir.dt.uint16
+U8 = mybir.dt.uint8
+FP8X4 = mybir.dt.float8_e4m3fn_x4
+ADD = mybir.AluOpType.add
+MULT = mybir.AluOpType.mult
+RELU = mybir.ActivationFunctionType.Relu
+
+P = 128
+PACK = 4
+PASSES = 2
+HALF = S // 2
+CHUNK = 256
+
+
+def tile_picked_devox_none_p_kernel(
+    tc, x_words, x_scales, w1, w2_words, w2_scales, gate, emb, offs, cell, pos1, pos2, out
+):
+    nc = tc.nc
+    with ExitStack() as ctx:
+        keep = ctx.enter_context(tc.tile_pool(name="keep", bufs=1))
+        psum = ctx.enter_context(tc.psum_pool(name="psum", bufs=1))
+
+        def sb(name, shape, dtype):
+            return keep.tile(shape, dtype, name=name, align_bytes=64)
+
+        def bank(b):
+            return psum.tile([P, 512], F32, name="bank%d" % b, tag="bank%d" % b)
+
+        offs_t = sb("offs_t", [P, S // 16], U16)
+        cell_t = sb("cell_t", [P, S // 16], U16)
+        pos_t = [sb("pos_t%d" % d, [P, V // 16], U16) for d in range(2)]
+        xs = sb("xs", [P, T], U8)
+        w2s = sb("w2s", [P, N], U8)
+        w1_raw = [sb("w1_raw%d" % z, [P, PACK, H], F32) for z in range(PASSES)]
+        xw = [sb("xw%d" % z, [P, T], U32) for z in range(PASSES)]
+        emb_t = [sb("emb_t%d" % t, [P, U], F32) for t in range(PACK)]
+        w2w = sb("w2w", [P, N], U32)
+        gate_t = sb("gate_t", [P, 2, V], F32)
+        up = [sb("up%d" % t, [P, U], F32) for t in range(PACK)]
+
+        nc.vector.memset(xs[:].bitcast(I32), 0)
+        nc.vector.memset(w2s[:].bitcast(I32), 0)
+        nc.sync.dma_start(offs_t[:], offs)
+        for z in range(PASSES):
+            nc.sync.dma_start(
+                out=w1_raw[z][:], in_=w1[512 * z : 512 * (z + 1), :].rearrange("(p j) c -> p j c", j=PACK)
+            )
+            if z == 0:
+                for q in range(4):
+                    nc.sync.dma_start(
+                        out=xs[32 * q : 32 * q + 8, :].bitcast(I32),
+                        in_=x_scales[:, 4 * q : 4 * q + 4, :].bitcast(I32),
+                    )
+        nc.sync.dma_start(cell_t[:], cell)
+        for z in range(PASSES):
+            nc.sync.dma_start(
+                out=xw[z][:].bitcast(I32), in_=x_words[z].rearrange("p n t -> p (n t)").bitcast(I32)
+            )
+        emb_v = emb.rearrange("(p t) r -> p t r", t=PACK)
+        for t in (3, 1, 0, 2):
+            nc.sync.dma_start(out=emb_t[t][:], in_=emb_v[:, t, :])
+        nc.sync.dma_start(out=w2w[:].bitcast(I32), in_=w2_words[0].rearrange("p n t -> p (n t)").bitcast(I32))
+        for q in range(4):
+            nc.sync.dma_start(
+                out=w2s[32 * q : 32 * q + 4, :].bitcast(I32),
+                in_=w2_scales[0, 4 * q : 4 * q + 4, :].bitcast(I32),
+            )
+        nc.sync.dma_start(out=gate_t[:], in_=gate.rearrange("d p v -> p d v"))
+        nc.sync.dma_start(pos_t[0][:], pos1)
+        nc.sync.dma_start(pos_t[1][:], pos2)
+
+        for t in (1, 3):
+            nc.vector.memset(up[t][:], 0.0)
+        for t in (0, 2):
+            nc.gpsimd.memset(up[t][:], 0.0)
+        ident = sb("ident", [P, P], F32)
+        make_identity(nc, ident[:])
+        zt = [[sb("zt%d_%d" % (u, a), [P, 4, P, 2], BF16) for a in range(2)] for u in range(2)]
+        for a in range(2):
+            nc.gpsimd.memset(zt[1][a][:].rearrange("p b q e -> p (b q e)").bitcast(F32), 0.0)
+
+        w1c = [[None, None] for z in range(PASSES)]
+        w1s = [[None, None] for z in range(PASSES)]
+        xs_g = sb("xs_g", [P, S], U8)
+        for z in range(PASSES):
+            src = w1_raw[z][:].rearrange("p j (m t) -> p m j t", t=PACK)
+            grouped = [sb("w1g%d_%d" % (z, u), [P, 2 * P * PACK], BF16) for u in range(2)]
+            nc.scalar.copy(
+                out=grouped[1][:].rearrange("p (t m j) -> p m j t", t=2, j=PACK), in_=src[:, :, :, 2:4]
+            )
+            nc.vector.tensor_copy(
+                out=grouped[0][:].rearrange("p (t m j) -> p m j t", t=2, j=PACK), in_=src[:, :, :, 0:2]
+            )
+            if z == 0:
+                nc.vector.tensor_copy(out=xs_g[:], in_=xs[:].indirect(offs_t[:]))
+            for u in range(2):
+                w1c[z][u] = sb("w1c%d_%d" % (z, u), [P, 2 * P], U32)
+                w1s[z][u] = sb("w1s%d_%d" % (z, u), [P, 2 * P], U8)
+                nc.vector.quantize_mx(out=w1c[z][u][:].bitcast(FP8X4), scales=w1s[z][u][:], in_=grouped[u][:])
+
+        xg0 = sb("xg0", [P, S], U32)
+        nc.vector.tensor_copy(out=xg0[:], in_=xw[0][:].indirect(offs_t[:]))
+        xg1 = sb("xg1", [P, S], U32)
+        for a in range(2):
+            nc.vector.tensor_copy(
+                out=xg1[:, a * HALF : (a + 1) * HALF], in_=xw[1][:].indirect(offs_t[:, 16 * a : 16 * (a + 1)])
+            )
+        xg = [xg0, xg1]
+
+        def first_product(b, t, lo, hi):
+            acc = bank(b)
+            u, e = divmod(t, 2)
+            for z in range(PASSES):
+                nc.tensor.matmul_mx(
+                    out=acc[:, 0 : hi - lo],
+                    lhsT=w1c[z][u][:, e * P : (e + 1) * P].bitcast(FP8X4),
+                    lhsT_scale=w1s[z][u][:, e * P : (e + 1) * P],
+                    rhs=xg[z][:, lo:hi].bitcast(FP8X4),
+                    rhs_scale=xs_g[4 * z : P, lo:hi],
+                    start=(z == 0),
+                    stop=(z == PASSES - 1),
+                )
+            h = sb("h%d_%d" % (t, lo), [P, hi - lo], F32)
+            nc.scalar.activation(out=h[:], in_=acc[:, 0 : hi - lo], func=RELU)
+            return h
+
+        pieces = [(1, 0, HALF), (3, 0, S), (1, HALF, S), (0, 0, S), (2, 0, S)]
+        hs = [first_product(b, t, lo, hi) for b, (t, lo, hi) in enumerate(pieces)]
+
+        def scatter(n):
+            t, lo, hi = pieces[n]
+            nc.vector.tensor_copy(out=up[t][:].indirect(cell_t[:, lo // 16 : hi // 16]), in_=hs[n][:])
+
+        nchunk = U // CHUNK
+        pr = [sb("pr%d" % c, [P, 2, CHUNK, 2], BF16) for c in range(nchunk)]
+
+        def turn(acc, src, a, first, last):
+            for b in range(4):
+                lo = 512 * a + P * b
+                nc.tensor.matmul(
+                    acc[:, b * P : (b + 1) * P],
+                    lhsT=src[:, lo : lo + P],
+                    rhs=ident[:],
+                    is_transpose=True,
+                    start=(first and b == 0),
+                    stop=(last and b == 3),
+                )
+
+        def open_sum(b, t, a):
+            acc = bank(b)
+            turn(acc, emb_t[t], a, True, False)
+            return acc
+
+        def close_sum(acc, t, a):
+            turn(acc, up[t], a, False, True)
+            u, e = divmod(t, 2)
+            nc.scalar.copy(out=zt[u][a][:, :, :, e], in_=acc[:].rearrange("p (b q) -> p b q", b=4))
+
+        def turn_back(b, u, a):
+            acc = bank(b)
+            words = zt[u][a][:].rearrange("p b q e -> p (b q e)").bitcast(F32)
+            for i in range(4):
+                nc.tensor.transpose(acc[:, i * P : (i + 1) * P], words[:, i * P : (i + 1) * P], ident[:])
+            for i in range(2):
+                dst = pr[2 * a + i][:, u, :, :].rearrange("p r e -> p (r e)").bitcast(F32)
+                nc.scalar.copy(out=dst, in_=acc[:, i * CHUNK : (i + 1) * CHUNK])
+
+        for n in range(len(pieces)):
+            scatter(n)
+        sums3 = [open_sum(5 + a, 3, a) for a in range(2)]
+        sums1 = [open_sum((7, 0)[a], 1, a) for a in range(2)]
+        for a in range(2):
+            close_sum(sums3[a], 3, a)
+        sums0 = [open_sum(3 + a, 0, a) for a in range(2)]
+        for a in range(2):
+            turn_back(1 + a, 1, a)
+        for a in range(2):
+            close_sum(sums1[a], 1, a)
+        for a in range(2):
+            close_sum(sums0[a], 0, a)
+        for a in range(2):
+            turn_back(5 + a, 0, a)
+
+        y = sb("y", [P, U], F32)
+        zq = []
+        for c in range(nchunk):
+            cols = slice(c * CHUNK, (c + 1) * CHUNK)
+            nc.vector.tensor_tensor(out=pr[c][:, 1, :, 0], in0=up[2][:, cols], in1=emb_t[2][:, cols], op=ADD)
+            zi = sb("zi%d" % c, [P, CHUNK * PACK], BF16)
+            words = pr[c][:].rearrange("p u r e -> p (u r e)").bitcast(F32).rearrange("p (u r) -> p r u", u=2)
+            dst = zi[:].bitcast(F32).rearrange("p (r u) -> p r u", u=2)
+            if c < nchunk - 1:
+                nc.scalar.copy(out=dst, in_=words)
+            else:
+                nc.vector.tensor_copy(out=dst, in_=words)
+            zq.append(zi)
+        acc01 = bank(7)
+        for c in (0, 1, 3, 2):
+            cols = slice(c * CHUNK, (c + 1) * CHUNK)
+            zc = sb("zc%d" % c, [P, CHUNK], U32)
+            zs = sb("zs%d" % c, [P, CHUNK], U8)
+            nc.vector.quantize_mx(out=zc[:].bitcast(FP8X4), scales=zs[:], in_=zq[c][:])
+            if c < 2:
+                res = acc01[:, cols]
+            else:
+                acc = bank(c - 2)
+                res = acc[:, 0:CHUNK]
+            nc.tensor.matmul_mx(
+                out=res,
+                lhsT=w2w[:].bitcast(FP8X4),
+                lhsT_scale=w2s[:],
+                rhs=zc[:].bitcast(FP8X4),
+                rhs_scale=zs[:],
+                start=True,
+                stop=True,
+            )
+            if c == 1:
+                nc.scalar.copy(out=y[:, 0 : 2 * CHUNK], in_=acc01[:])
+            elif c == 3:
+                nc.scalar.copy(out=y[:, cols], in_=res)
+            elif c == 2:
+                nc.vector.tensor_copy(out=y[:, cols], in_=res)
+
+        spans = [(0, 384), (384, 512)]
+        g = [[sb("g%d_%d" % (a, d), [P, hi - lo], F32) for d in range(2)] for a, (lo, hi) in enumerate(spans)]
+
+        def fetch(a, d):
+            lo, hi = spans[a]
+            nc.vector.tensor_tensor(
+                out=g[a][d][:], in0=y[:].indirect(pos_t[d][:, lo // 16 : hi // 16]), in1=gate_t[:, d, lo:hi], op=MULT
+            )
+
+        def finish(a):
+            lo, hi = spans[a]
+            o = sb("o%d" % a, [P, hi - lo], F32)
+            nc.vector.tensor_tensor(out=o[:], in0=g[a][0][:], in1=g[a][1][:], op=ADD)
+            nc.sync.dma_start(out=out[:, lo:hi], in_=o[:])
+
+        fetch(0, 0)
+        fetch(0, 1)
+        fetch(1, 0)
+        finish(0)
+        fetch(1, 1)
+        finish(1)

@@ -1,7 +1,6 @@
 from contextlib import ExitStack
 
 import concourse.mybir as mybir
-from concourse.masks import make_identity
 
 K, T, S, V, H, N, U = 1024, 2048, 512, 512, 512, 128, 1024
 FLOPS = 2 * K * H * S + 2 * H * N * U
@@ -48,7 +47,8 @@ def tile_picked_devox_none_p_kernel(
         emb_t = [sb("emb_t%d" % t, [P, U], F32) for t in range(PACK)]
         w2w = sb("w2w", [P, N], U32)
         gate_t = sb("gate_t", [P, 2, V], F32)
-        up = [sb("up%d" % t, [P, U], F32) for t in range(PACK)]
+        win = [sb("win%d" % n, [P, U], F32) for n in range(3)]
+        up = [win[0], win[1], win[2], win[2]]
 
         nc.vector.memset(xs[:].bitcast(I32), 0)
         nc.vector.memset(w2s[:].bitcast(I32), 0)
@@ -69,7 +69,7 @@ def tile_picked_devox_none_p_kernel(
                 out=xw[z][:].bitcast(I32), in_=x_words[z].rearrange("p n t -> p (n t)").bitcast(I32)
             )
         emb_v = emb.rearrange("(p t) r -> p t r", t=PACK)
-        for t in (3, 1, 0, 2):
+        for t in (1, 3, 0, 2):
             nc.sync.dma_start(out=emb_t[t][:], in_=emb_v[:, t, :])
         nc.sync.dma_start(out=w2w[:].bitcast(I32), in_=w2_words[0].rearrange("p n t -> p (n t)").bitcast(I32))
         for q in range(4):
@@ -81,15 +81,8 @@ def tile_picked_devox_none_p_kernel(
         nc.sync.dma_start(pos_t[0][:], pos1)
         nc.sync.dma_start(pos_t[1][:], pos2)
 
-        for t in (1, 3):
-            nc.vector.memset(up[t][:], 0.0)
-        for t in (0, 2):
-            nc.gpsimd.memset(up[t][:], 0.0)
-        ident = sb("ident", [P, P], F32)
-        make_identity(nc, ident[:])
-        zt = [[sb("zt%d_%d" % (u, a), [P, 4, P, 2], BF16) for a in range(2)] for u in range(2)]
-        for a in range(2):
-            nc.gpsimd.memset(zt[1][a][:].rearrange("p b q e -> p (b q e)").bitcast(F32), 0.0)
+        for n in range(3):
+            nc.vector.memset(win[n][:], 0.0)
 
         w1c = [[None, None] for z in range(PASSES)]
         w1s = [[None, None] for z in range(PASSES)]
@@ -136,7 +129,7 @@ def tile_picked_devox_none_p_kernel(
             nc.scalar.activation(out=h[:], in_=acc[:, 0 : hi - lo], func=RELU)
             return h
 
-        pieces = [(1, 0, HALF), (3, 0, S), (1, HALF, S), (0, 0, S), (2, 0, S)]
+        pieces = [(1, 0, HALF), (1, HALF, S), (3, 0, S), (0, 0, S), (2, 0, S)]
         hs = [first_product(b, t, lo, hi) for b, (t, lo, hi) in enumerate(pieces)]
 
         def scatter(n):
@@ -146,52 +139,16 @@ def tile_picked_devox_none_p_kernel(
         nchunk = U // CHUNK
         pr = [sb("pr%d" % c, [P, 2, CHUNK, 2], BF16) for c in range(nchunk)]
 
-        def turn(acc, src, a, first, last):
-            for b in range(4):
-                lo = 512 * a + P * b
-                nc.tensor.matmul(
-                    acc[:, b * P : (b + 1) * P],
-                    lhsT=src[:, lo : lo + P],
-                    rhs=ident[:],
-                    is_transpose=True,
-                    start=(first and b == 0),
-                    stop=(last and b == 3),
-                )
-
-        def open_sum(b, t, a):
-            acc = bank(b)
-            turn(acc, emb_t[t], a, True, False)
-            return acc
-
-        def close_sum(acc, t, a):
-            turn(acc, up[t], a, False, True)
+        def add_plane(t):
             u, e = divmod(t, 2)
-            nc.scalar.copy(out=zt[u][a][:, :, :, e], in_=acc[:].rearrange("p (b q) -> p b q", b=4))
-
-        def turn_back(b, u, a):
-            acc = bank(b)
-            words = zt[u][a][:].rearrange("p b q e -> p (b q e)").bitcast(F32)
-            for i in range(4):
-                nc.tensor.transpose(acc[:, i * P : (i + 1) * P], words[:, i * P : (i + 1) * P], ident[:])
-            for i in range(2):
-                dst = pr[2 * a + i][:, u, :, :].rearrange("p r e -> p (r e)").bitcast(F32)
-                nc.scalar.copy(out=dst, in_=acc[:, i * CHUNK : (i + 1) * CHUNK])
+            for c in range(nchunk):
+                cols = slice(c * CHUNK, (c + 1) * CHUNK)
+                nc.gpsimd.tensor_tensor(out=pr[c][:, u, :, e], in0=up[t][:, cols], in1=emb_t[t][:, cols], op=ADD)
 
         for n in range(len(pieces)):
             scatter(n)
-        sums3 = [open_sum(5 + a, 3, a) for a in range(2)]
-        sums1 = [open_sum((7, 0)[a], 1, a) for a in range(2)]
-        for a in range(2):
-            close_sum(sums3[a], 3, a)
-        sums0 = [open_sum(3 + a, 0, a) for a in range(2)]
-        for a in range(2):
-            turn_back(1 + a, 1, a)
-        for a in range(2):
-            close_sum(sums1[a], 1, a)
-        for a in range(2):
-            close_sum(sums0[a], 0, a)
-        for a in range(2):
-            turn_back(5 + a, 0, a)
+            if 0 < n < len(pieces) - 1:
+                add_plane(pieces[n][0])
 
         y = sb("y", [P, U], F32)
         zq = []

@@ -31,8 +31,8 @@ def tile_picked_devox_none_p_kernel(
         keep = ctx.enter_context(tc.tile_pool(name="keep", bufs=1))
         psum = ctx.enter_context(tc.psum_pool(name="psum", bufs=1))
 
-        def sb(name, shape, dtype):
-            return keep.tile(shape, dtype, name=name, align_bytes=64)
+        def sb(name, shape, dtype, tag=None):
+            return keep.tile(shape, dtype, name=name, tag=tag or name, align_bytes=64)
 
         def bank(b):
             return psum.tile([P, 512], F32, name="bank%d" % b, tag="bank%d" % b)
@@ -40,53 +40,46 @@ def tile_picked_devox_none_p_kernel(
         offs_t = sb("offs_t", [P, S // 16], U16)
         cell_t = sb("cell_t", [P, S // 16], U16)
         pos_t = [sb("pos_t%d" % d, [P, V // 16], U16) for d in range(2)]
-        xs = sb("xs", [P, T], U8)
-        w2s = sb("w2s", [P, N], U8)
+        xs = sb("xs", [P, PASSES * T], U8)
         w1_raw = [sb("w1_raw%d" % z, [P, PACK, H], F32) for z in range(PASSES)]
         xw = [sb("xw%d" % z, [P, T], U32) for z in range(PASSES)]
-        emb_t = [sb("emb_t%d" % t, [P, U], F32) for t in range(PACK)]
-        w2w = sb("w2w", [P, N], U32)
-        gate_t = sb("gate_t", [P, 2, V], F32)
         win = [sb("win%d" % n, [P, U], F32) for n in range(3)]
-        up = [win[0], win[1], win[2], win[2]]
+        up = [win[1], win[0], win[0], win[2]]
 
         nc.vector.memset(xs[:].bitcast(I32), 0)
-        nc.vector.memset(w2s[:].bitcast(I32), 0)
         nc.sync.dma_start(offs_t[:], offs)
         for z in range(PASSES):
             nc.sync.dma_start(
                 out=w1_raw[z][:], in_=w1[512 * z : 512 * (z + 1), :].rearrange("(p j) c -> p j c", j=PACK)
             )
             if z == 0:
-                for q in range(4):
-                    nc.sync.dma_start(
-                        out=xs[32 * q : 32 * q + 8, :].bitcast(I32),
-                        in_=x_scales[:, 4 * q : 4 * q + 4, :].bitcast(I32),
-                    )
-        nc.sync.dma_start(cell_t[:], cell)
+                nc.sync.dma_start(
+                    out=xs[0:P:8, :].bitcast(I32).rearrange("q (z n) -> q z n", z=PASSES),
+                    in_=x_scales.rearrange("z q n -> q z n").bitcast(I32),
+                )
         for z in range(PASSES):
             nc.sync.dma_start(
                 out=xw[z][:].bitcast(I32), in_=x_words[z].rearrange("p n t -> p (n t)").bitcast(I32)
             )
-        emb_v = emb.rearrange("(p t) r -> p t r", t=PACK)
-        for t in (1, 3, 0, 2):
-            nc.sync.dma_start(out=emb_t[t][:], in_=emb_v[:, t, :])
-        nc.sync.dma_start(out=w2w[:].bitcast(I32), in_=w2_words[0].rearrange("p n t -> p (n t)").bitcast(I32))
-        for q in range(4):
-            nc.sync.dma_start(
-                out=w2s[32 * q : 32 * q + 4, :].bitcast(I32),
-                in_=w2_scales[0, 4 * q : 4 * q + 4, :].bitcast(I32),
-            )
-        nc.sync.dma_start(out=gate_t[:], in_=gate.rearrange("d p v -> p d v"))
+        nc.sync.dma_start(cell_t[:], cell)
         nc.sync.dma_start(pos_t[0][:], pos1)
         nc.sync.dma_start(pos_t[1][:], pos2)
 
-        for n in range(3):
-            nc.vector.memset(win[n][:], 0.0)
+        nc.vector.memset(win[0][:], 0.0)
+        for n in (1, 2):
+            nc.gpsimd.memset(win[n][:], 0.0)
 
         w1c = [[None, None] for z in range(PASSES)]
         w1s = [[None, None] for z in range(PASSES)]
-        xs_g = sb("xs_g", [P, S], U8)
+        xs_g = sb("xs_g", [P, PASSES * S], U8)
+        for z in range(PASSES):
+            nc.vector.tensor_copy(
+                out=xs_g[:, z * S : (z + 1) * S], in_=xs[:, z * T : (z + 1) * T].indirect(offs_t[:])
+            )
+        xs_at = sb("xs_at", [P, PASSES * S], U8)
+        nc.vector.tensor_copy(out=xs_at[:], in_=xs_g[:])
+        for r in range(1, 4):
+            nc.sync.dma_start(out=xs_at[r:P:32, :].bitcast(I32), in_=xs_g[8 * r : P : 32, :].bitcast(I32))
         for z in range(PASSES):
             src = w1_raw[z][:].rearrange("p j (m t) -> p m j t", t=PACK)
             grouped = [sb("w1g%d_%d" % (z, u), [P, 2 * P * PACK], BF16) for u in range(2)]
@@ -96,8 +89,6 @@ def tile_picked_devox_none_p_kernel(
             nc.vector.tensor_copy(
                 out=grouped[0][:].rearrange("p (t m j) -> p m j t", t=2, j=PACK), in_=src[:, :, :, 0:2]
             )
-            if z == 0:
-                nc.vector.tensor_copy(out=xs_g[:], in_=xs[:].indirect(offs_t[:]))
             for u in range(2):
                 w1c[z][u] = sb("w1c%d_%d" % (z, u), [P, 2 * P], U32)
                 w1s[z][u] = sb("w1s%d_%d" % (z, u), [P, 2 * P], U8)
@@ -111,71 +102,104 @@ def tile_picked_devox_none_p_kernel(
                 out=xg1[:, a * HALF : (a + 1) * HALF], in_=xw[1][:].indirect(offs_t[:, 16 * a : 16 * (a + 1)])
             )
         xg = [xg0, xg1]
+        emb_v = emb.rearrange("(p t) r -> p t r", t=PACK)
+        emb_t = [sb("emb_t%d" % t, [P, U], F32, ("xw1", "xw0", "w1_raw1")[t]) for t in range(3)]
+        for t in (1, 0, 2):
+            nc.sync.dma_start(out=emb_t[t][:], in_=emb_v[:, t, :])
 
-        def first_product(b, t, lo, hi):
-            acc = bank(b)
+        def first_product(acc, at, t, lo, hi):
             u, e = divmod(t, 2)
             for z in range(PASSES):
                 nc.tensor.matmul_mx(
-                    out=acc[:, 0 : hi - lo],
+                    out=acc[:, at : at + hi - lo],
                     lhsT=w1c[z][u][:, e * P : (e + 1) * P].bitcast(FP8X4),
                     lhsT_scale=w1s[z][u][:, e * P : (e + 1) * P],
                     rhs=xg[z][:, lo:hi].bitcast(FP8X4),
-                    rhs_scale=xs_g[4 * z : P, lo:hi],
+                    rhs_scale=xs_at[:, z * S + lo : z * S + hi],
                     start=(z == 0),
                     stop=(z == PASSES - 1),
                 )
-            h = sb("h%d_%d" % (t, lo), [P, hi - lo], F32)
-            nc.scalar.activation(out=h[:], in_=acc[:, 0 : hi - lo], func=RELU)
+
+        def rectify(t, src, lo):
+            h = sb("h%d_%d" % (t, lo), [P, src.shape[1]], F32)
+            nc.scalar.activation(out=h[:], in_=src, func=RELU)
             return h
 
-        pieces = [(1, 0, HALF), (1, HALF, S), (3, 0, S), (0, 0, S), (2, 0, S)]
-        hs = [first_product(b, t, lo, hi) for b, (t, lo, hi) in enumerate(pieces)]
-
-        def scatter(n):
-            t, lo, hi = pieces[n]
-            nc.vector.tensor_copy(out=up[t][:].indirect(cell_t[:, lo // 16 : hi // 16]), in_=hs[n][:])
+        def place(t, h, lo, hi):
+            nc.vector.tensor_copy(out=up[t][:].indirect(cell_t[:, lo // 16 : hi // 16]), in_=h[:])
 
         nchunk = U // CHUNK
-        pr = [sb("pr%d" % c, [P, 2, CHUNK, 2], BF16) for c in range(nchunk)]
+
+        def halves(c, t):
+            u, e = divmod(t, 2)
+            words = pairs[c][:, u * CHUNK : (u + 1) * CHUNK]
+            return words.bitcast(BF16).rearrange("p (r e) -> p r e", e=2)[:, :, e]
 
         def add_plane(t):
-            u, e = divmod(t, 2)
             for c in range(nchunk):
                 cols = slice(c * CHUNK, (c + 1) * CHUNK)
-                nc.gpsimd.tensor_tensor(out=pr[c][:, u, :, e], in0=up[t][:, cols], in1=emb_t[t][:, cols], op=ADD)
+                other = pairs[c][:, CHUNK:] if t == 3 else emb_t[t][:, cols]
+                nc.gpsimd.tensor_tensor(out=halves(c, t), in0=up[t][:, cols], in1=other, op=ADD)
 
-        for n in range(len(pieces)):
-            scatter(n)
-            if 0 < n < len(pieces) - 1:
-                add_plane(pieces[n][0])
+        acc = bank(0)
+        first_product(acc, 0, 1, 0, 128)
+        place(1, rectify(1, acc[:, 0:128], 0), 0, 128)
+        acc = bank(1)
+        first_product(acc, 0, 1, 128, 256)
+        first_product(acc, 128, 1, 256, 512)
+        place(1, rectify(1, acc[:, 0:384], 128), 128, 512)
+        hs = {}
+        for b, t in enumerate((0, 3, 2)):
+            acc = bank(2 + b)
+            first_product(acc, 0, t, 0, S)
+            hs[t] = rectify(t, acc[:], 0)
+
+        pairs = [sb("pairs%d" % c, [P, 2 * CHUNK], F32, "w1c%d_%d" % divmod(c, 2)) for c in range(nchunk)]
+        for c in range(nchunk):
+            nc.sync.dma_start(out=pairs[c][:, CHUNK:], in_=emb_v[:, 3, c * CHUNK : (c + 1) * CHUNK])
+        w2w = sb("w2w", [P, N], U32, "xg1")
+        nc.sync.dma_start(out=w2w[:].bitcast(I32), in_=w2_words[0].rearrange("p n t -> p (n t)").bitcast(I32))
+        w2s = sb("w2s", [P, N], U8, "w1s0_0")
+        nc.gpsimd.memset(w2s[:].bitcast(I32), 0)
+        for q in range(4):
+            nc.sync.dma_start(
+                out=w2s[32 * q : 32 * q + 4, :].bitcast(I32),
+                in_=w2_scales[0, 4 * q : 4 * q + 4, :].bitcast(I32),
+            )
+        gate_t = sb("gate_t", [P, 2, V], F32, "xg0")
+        nc.sync.dma_start(out=gate_t[:], in_=gate.rearrange("d p v -> p d v"))
+
+        add_plane(1)
+        for t in (0, 3, 2):
+            place(t, hs[t], 0, S)
+            if t != 2:
+                add_plane(t)
+
+        def quantise(name, src, width):
+            codes = sb("c" + name, [P, width], U32)
+            scales = sb("s" + name, [P, width], U8)
+            nc.vector.quantize_mx(out=codes[:].bitcast(FP8X4), scales=scales[:], in_=src)
+            return codes, scales
 
         y = sb("y", [P, U], F32)
+        edges = (0, 256, 512, 768, 1024)
+        chunks = [slice(lo, hi) for lo, hi in zip(edges, edges[1:])]
         zq = []
-        for c in range(nchunk):
-            cols = slice(c * CHUNK, (c + 1) * CHUNK)
-            nc.vector.tensor_tensor(out=pr[c][:, 1, :, 0], in0=up[2][:, cols], in1=emb_t[2][:, cols], op=ADD)
-            zi = sb("zi%d" % c, [P, CHUNK * PACK], BF16)
-            words = pr[c][:].rearrange("p u r e -> p (u r e)").bitcast(F32).rearrange("p (u r) -> p r u", u=2)
-            dst = zi[:].bitcast(F32).rearrange("p (r u) -> p r u", u=2)
-            if c < nchunk - 1:
-                nc.scalar.copy(out=dst, in_=words)
-            else:
-                nc.vector.tensor_copy(out=dst, in_=words)
+        for c, cols in enumerate(chunks):
+            width = cols.stop - cols.start
+            nc.vector.tensor_tensor(out=halves(c, 2), in0=up[2][:, cols], in1=emb_t[2][:, cols], op=ADD)
+            zi = sb("zi%d" % c, [P, width * PACK], BF16)
+            words = pairs[c][:].rearrange("p (u r) -> p r u", u=2)
+            weave = nc.vector.tensor_copy if c in () else nc.scalar.copy
+            weave(out=zi[:].bitcast(F32).rearrange("p (r u) -> p r u", u=2), in_=words)
             zq.append(zi)
-        acc01 = bank(7)
-        for c in (0, 1, 3, 2):
-            cols = slice(c * CHUNK, (c + 1) * CHUNK)
-            zc = sb("zc%d" % c, [P, CHUNK], U32)
-            zs = sb("zs%d" % c, [P, CHUNK], U8)
-            nc.vector.quantize_mx(out=zc[:].bitcast(FP8X4), scales=zs[:], in_=zq[c][:])
-            if c < 2:
-                res = acc01[:, cols]
-            else:
-                acc = bank(c - 2)
-                res = acc[:, 0:CHUNK]
+        for c in (0, 1, 2, 3):
+            cols = chunks[c]
+            width = cols.stop - cols.start
+            zc, zs = quantise("z%d" % c, zq[c][:], width)
+            acc = bank((5, 6, 7, 0)[c])
             nc.tensor.matmul_mx(
-                out=res,
+                out=acc[:, 0:width],
                 lhsT=w2w[:].bitcast(FP8X4),
                 lhsT_scale=w2s[:],
                 rhs=zc[:].bitcast(FP8X4),
@@ -183,12 +207,8 @@ def tile_picked_devox_none_p_kernel(
                 start=True,
                 stop=True,
             )
-            if c == 1:
-                nc.scalar.copy(out=y[:, 0 : 2 * CHUNK], in_=acc01[:])
-            elif c == 3:
-                nc.scalar.copy(out=y[:, cols], in_=res)
-            elif c == 2:
-                nc.vector.tensor_copy(out=y[:, cols], in_=res)
+            leave = nc.vector.tensor_copy if c in (3,) else nc.scalar.copy
+            leave(out=y[:, cols], in_=acc[:, 0:width])
 
         spans = [(0, 384), (384, 512)]
         g = [[sb("g%d_%d" % (a, d), [P, hi - lo], F32) for d in range(2)] for a, (lo, hi) in enumerate(spans)]

@@ -190,10 +190,10 @@ def tile_picked_devox_none_p_kernel(
             nc.vector.tensor_tensor(out=halves(c, 2), in0=up[2][:, cols], in1=emb_t[2][:, cols], op=ADD)
             zi = sb("zi%d" % c, [P, width * PACK], BF16)
             words = pairs[c][:].rearrange("p (u r) -> p r u", u=2)
-            weave = nc.vector.tensor_copy if c in () else nc.scalar.copy
+            weave = nc.vector.tensor_copy if c in (3,) else nc.scalar.copy
             weave(out=zi[:].bitcast(F32).rearrange("p (r u) -> p r u", u=2), in_=words)
             zq.append(zi)
-        for c in (0, 1, 2, 3):
+        for c in (0, 1, 3, 2):
             cols = chunks[c]
             width = cols.stop - cols.start
             zc, zs = quantise("z%d" % c, zq[c][:], width)
@@ -207,7 +207,7 @@ def tile_picked_devox_none_p_kernel(
                 start=True,
                 stop=True,
             )
-            leave = nc.vector.tensor_copy if c in (3,) else nc.scalar.copy
+            leave = nc.vector.tensor_copy if c in (2,) else nc.scalar.copy
             leave(out=y[:, cols], in_=acc[:, 0:width])
 
         spans = [(0, 384), (384, 512)]

@@ -21,6 +21,8 @@ PACK = 4
 PASSES = 2
 HALF = S // 2
 CHUNK = 256
+FIRST = 128
+ORDER = (0, 1, 3, 2)
 
 
 def tile_picked_devox_none_p_kernel(
@@ -40,31 +42,31 @@ def tile_picked_devox_none_p_kernel(
         offs_t = sb("offs_t", [P, S // 16], U16)
         cell_t = sb("cell_t", [P, S // 16], U16)
         pos_t = [sb("pos_t%d" % d, [P, V // 16], U16) for d in range(2)]
-        xs = sb("xs", [P, PASSES * T], U8)
+        xs = sb("xs", [P, PASSES * T], U8, "xw1")
         w1_raw = [sb("w1_raw%d" % z, [P, PACK, H], F32) for z in range(PASSES)]
-        xw = [sb("xw%d" % z, [P, T], U32) for z in range(PASSES)]
+        xw = [sb("xw0", [P, T], U32)]
         win = [sb("win%d" % n, [P, U], F32) for n in range(3)]
         up = [win[1], win[0], win[0], win[2]]
 
-        nc.vector.memset(xs[:].bitcast(I32), 0)
+        nc.gpsimd.memset(xs[:, :T].bitcast(I32), 0)
+        nc.vector.memset(xs[:, T:].bitcast(I32), 0)
+        w1_v = [w1[512 * z : 512 * (z + 1), :].rearrange("(p j) c -> p j c", j=PACK) for z in range(PASSES)]
+        nc.sync.dma_start(out=w1_raw[0][:, 0:2, :], in_=w1_v[0][:, 0:2, :])
+        nc.sync.dma_start(
+            out=xs[0:P:8, :].bitcast(I32).rearrange("q (z n) -> q z n", z=PASSES),
+            in_=x_scales.rearrange("z q n -> q z n").bitcast(I32),
+        )
         nc.sync.dma_start(offs_t[:], offs)
-        for z in range(PASSES):
-            nc.sync.dma_start(
-                out=w1_raw[z][:], in_=w1[512 * z : 512 * (z + 1), :].rearrange("(p j) c -> p j c", j=PACK)
-            )
-            if z == 0:
-                nc.sync.dma_start(
-                    out=xs[0:P:8, :].bitcast(I32).rearrange("q (z n) -> q z n", z=PASSES),
-                    in_=x_scales.rearrange("z q n -> q z n").bitcast(I32),
-                )
-        for z in range(PASSES):
-            nc.sync.dma_start(
-                out=xw[z][:].bitcast(I32), in_=x_words[z].rearrange("p n t -> p (n t)").bitcast(I32)
-            )
         nc.sync.dma_start(cell_t[:], cell)
         nc.sync.dma_start(pos_t[0][:], pos1)
         nc.sync.dma_start(pos_t[1][:], pos2)
+        nc.sync.dma_start(out=w1_raw[0][:, 2:4, :], in_=w1_v[0][:, 2:4, :])
+        x_v = [x_words[z].rearrange("p n t -> p (n t)").bitcast(I32) for z in range(PASSES)]
+        nc.sync.dma_start(out=xw[0][:].bitcast(I32), in_=x_v[0])
+        nc.sync.dma_start(out=w1_raw[1][:], in_=w1_v[1])
 
+        xs_at = sb("xs_at", [P, PASSES * S], U8)
+        nc.vector.memset(xs_at[:].bitcast(I32), 0)
         nc.vector.memset(win[0][:], 0.0)
         for n in (1, 2):
             nc.gpsimd.memset(win[n][:], 0.0)
@@ -76,10 +78,10 @@ def tile_picked_devox_none_p_kernel(
             nc.vector.tensor_copy(
                 out=xs_g[:, z * S : (z + 1) * S], in_=xs[:, z * T : (z + 1) * T].indirect(offs_t[:])
             )
-        xs_at = sb("xs_at", [P, PASSES * S], U8)
-        nc.vector.tensor_copy(out=xs_at[:], in_=xs_g[:])
-        for r in range(1, 4):
+        for r in range(4):
             nc.sync.dma_start(out=xs_at[r:P:32, :].bitcast(I32), in_=xs_g[8 * r : P : 32, :].bitcast(I32))
+        xw.append(sb("xw1", [P, T], U32))
+        nc.sync.dma_start(out=xw[1][:].bitcast(I32), in_=x_v[1])
         for z in range(PASSES):
             src = w1_raw[z][:].rearrange("p j (m t) -> p m j t", t=PACK)
             grouped = [sb("w1g%d_%d" % (z, u), [P, 2 * P * PACK], BF16) for u in range(2)]
@@ -93,9 +95,10 @@ def tile_picked_devox_none_p_kernel(
                 w1c[z][u] = sb("w1c%d_%d" % (z, u), [P, 2 * P], U32)
                 w1s[z][u] = sb("w1s%d_%d" % (z, u), [P, 2 * P], U8)
                 nc.vector.quantize_mx(out=w1c[z][u][:].bitcast(FP8X4), scales=w1s[z][u][:], in_=grouped[u][:])
+            if z == 0:
+                xg0 = sb("xg0", [P, S], U32)
+                nc.vector.tensor_copy(out=xg0[:], in_=xw[0][:].indirect(offs_t[:]))
 
-        xg0 = sb("xg0", [P, S], U32)
-        nc.vector.tensor_copy(out=xg0[:], in_=xw[0][:].indirect(offs_t[:]))
         xg1 = sb("xg1", [P, S], U32)
         for a in range(2):
             nc.vector.tensor_copy(
@@ -107,17 +110,18 @@ def tile_picked_devox_none_p_kernel(
         for t in (1, 0, 2):
             nc.sync.dma_start(out=emb_t[t][:], in_=emb_v[:, t, :])
 
-        def first_product(acc, at, t, lo, hi):
+        def first_product(acc, z, t, lo, hi):
             u, e = divmod(t, 2)
-            for z in range(PASSES):
+            cuts = [lo, HALF, hi] if lo == FIRST else [lo, hi]
+            for a, b in zip(cuts, cuts[1:]):
                 nc.tensor.matmul_mx(
-                    out=acc[:, at : at + hi - lo],
+                    out=acc[:, a - lo : b - lo],
                     lhsT=w1c[z][u][:, e * P : (e + 1) * P].bitcast(FP8X4),
                     lhsT_scale=w1s[z][u][:, e * P : (e + 1) * P],
-                    rhs=xg[z][:, lo:hi].bitcast(FP8X4),
-                    rhs_scale=xs_at[:, z * S + lo : z * S + hi],
-                    start=(z == 0),
-                    stop=(z == PASSES - 1),
+                    rhs=xg[z][:, a:b].bitcast(FP8X4),
+                    rhs_scale=xs_at[:, z * S + a : z * S + b],
+                    start=(z == 0 and a == lo),
+                    stop=(z == PASSES - 1 and b == hi),
                 )
 
         def rectify(t, src, lo):
@@ -136,23 +140,21 @@ def tile_picked_devox_none_p_kernel(
             return words.bitcast(BF16).rearrange("p (r e) -> p r e", e=2)[:, :, e]
 
         def add_plane(t):
-            for c in range(nchunk):
+            for c in ORDER:
                 cols = slice(c * CHUNK, (c + 1) * CHUNK)
                 other = pairs[c][:, CHUNK:] if t == 3 else emb_t[t][:, cols]
                 nc.gpsimd.tensor_tensor(out=halves(c, t), in0=up[t][:, cols], in1=other, op=ADD)
 
-        acc = bank(0)
-        first_product(acc, 0, 1, 0, 128)
-        place(1, rectify(1, acc[:, 0:128], 0), 0, 128)
-        acc = bank(1)
-        first_product(acc, 0, 1, 128, 256)
-        first_product(acc, 128, 1, 256, 512)
-        place(1, rectify(1, acc[:, 0:384], 128), 128, 512)
+        pieces = [(1, 0, FIRST), (0, 0, FIRST), (1, FIRST, S), (0, FIRST, S), (3, 0, S), (2, 0, S)]
+        accs = [bank(b) for b in range(len(pieces))]
+        for acc, (t, lo, hi) in zip(accs, pieces):
+            first_product(acc, 0, t, lo, hi)
         hs = {}
-        for b, t in enumerate((0, 3, 2)):
-            acc = bank(2 + b)
-            first_product(acc, 0, t, 0, S)
-            hs[t] = rectify(t, acc[:], 0)
+        for acc, (t, lo, hi) in zip(accs, pieces):
+            first_product(acc, 1, t, lo, hi)
+            hs[t] = rectify(t, acc[:, 0 : hi - lo], lo)
+            if t < 2:
+                place(t, hs[t], lo, hi)
 
         pairs = [sb("pairs%d" % c, [P, 2 * CHUNK], F32, "w1c%d_%d" % divmod(c, 2)) for c in range(nchunk)]
         for c in range(nchunk):
@@ -170,7 +172,8 @@ def tile_picked_devox_none_p_kernel(
         nc.sync.dma_start(out=gate_t[:], in_=gate.rearrange("d p v -> p d v"))
 
         add_plane(1)
-        for t in (0, 3, 2):
+        add_plane(0)
+        for t in (3, 2):
             place(t, hs[t], 0, S)
             if t != 2:
                 add_plane(t)
@@ -184,31 +187,35 @@ def tile_picked_devox_none_p_kernel(
         y = sb("y", [P, U], F32)
         edges = (0, 256, 512, 768, 1024)
         chunks = [slice(lo, hi) for lo, hi in zip(edges, edges[1:])]
-        zq = []
-        for c, cols in enumerate(chunks):
-            width = cols.stop - cols.start
-            nc.vector.tensor_tensor(out=halves(c, 2), in0=up[2][:, cols], in1=emb_t[2][:, cols], op=ADD)
-            zi = sb("zi%d" % c, [P, width * PACK], BF16)
+        zq = {}
+        for c in ORDER:
+            nc.vector.tensor_tensor(out=halves(c, 2), in0=up[2][:, chunks[c]], in1=emb_t[2][:, chunks[c]], op=ADD)
+        for c in range(nchunk):
+            zq[c] = sb("zi%d" % c, [P, CHUNK * PACK], BF16)
             words = pairs[c][:].rearrange("p (u r) -> p r u", u=2)
-            weave = nc.vector.tensor_copy if c in (3,) else nc.scalar.copy
-            weave(out=zi[:].bitcast(F32).rearrange("p (r u) -> p r u", u=2), in_=words)
-            zq.append(zi)
-        for c in (0, 1, 3, 2):
-            cols = chunks[c]
-            width = cols.stop - cols.start
-            zc, zs = quantise("z%d" % c, zq[c][:], width)
-            acc = bank((5, 6, 7, 0)[c])
+            weave = nc.vector.tensor_copy if c == 3 else nc.scalar.copy
+            weave(out=zq[c][:].bitcast(F32).rearrange("p (r u) -> p r u", u=2), in_=words)
+
+        def second_product(b, zc, zs, at, lo, hi, leave):
+            acc = bank(b)
             nc.tensor.matmul_mx(
-                out=acc[:, 0:width],
+                out=acc[:, 0 : hi - lo],
                 lhsT=w2w[:].bitcast(FP8X4),
                 lhsT_scale=w2s[:],
-                rhs=zc[:].bitcast(FP8X4),
-                rhs_scale=zs[:],
+                rhs=zc[:, lo:hi].bitcast(FP8X4),
+                rhs_scale=zs[:, lo:hi],
                 start=True,
                 stop=True,
             )
-            leave = nc.vector.tensor_copy if c in (2,) else nc.scalar.copy
-            leave(out=y[:, cols], in_=acc[:, 0:width])
+            leave(out=y[:, at + lo : at + hi], in_=acc[:, 0 : hi - lo])
+
+        for c in ORDER:
+            zc, zs = quantise("z%d" % c, zq[c][:], CHUNK)
+            if c == ORDER[-1]:
+                second_product(1, zc, zs, c * CHUNK, 0, CHUNK // 2, nc.scalar.copy)
+                second_product(2, zc, zs, c * CHUNK, CHUNK // 2, CHUNK, nc.vector.tensor_copy)
+            else:
+                second_product((6, 7, None, 0)[c], zc, zs, c * CHUNK, 0, CHUNK, nc.scalar.copy)
 
         spans = [(0, 384), (384, 512)]
         g = [[sb("g%d_%d" % (a, d), [P, hi - lo], F32) for d in range(2)] for a, (lo, hi) in enumerate(spans)]

@@ -42,34 +42,33 @@ def tile_picked_devox_none_p_kernel(
         offs_t = sb("offs_t", [P, S // 16], U16)
         cell_t = sb("cell_t", [P, S // 16], U16)
         pos_t = [sb("pos_t%d" % d, [P, V // 16], U16) for d in range(2)]
-        xs = sb("xs", [P, PASSES * T], U8, "xw1")
+        xs = sb("xs", [P, PASSES * T], U8)
         w1_raw = [sb("w1_raw%d" % z, [P, PACK, H], F32) for z in range(PASSES)]
-        xw = [sb("xw0", [P, T], U32)]
+        xw = [sb("xw%d" % z, [P, T], U32) for z in range(PASSES)]
         win = [sb("win%d" % n, [P, U], F32) for n in range(3)]
         up = [win[1], win[0], win[0], win[2]]
 
-        nc.gpsimd.memset(xs[:, :T].bitcast(I32), 0)
-        nc.vector.memset(xs[:, T:].bitcast(I32), 0)
-        w1_v = [w1[512 * z : 512 * (z + 1), :].rearrange("(p j) c -> p j c", j=PACK) for z in range(PASSES)]
-        nc.sync.dma_start(out=w1_raw[0][:, 0:2, :], in_=w1_v[0][:, 0:2, :])
-        nc.sync.dma_start(
-            out=xs[0:P:8, :].bitcast(I32).rearrange("q (z n) -> q z n", z=PASSES),
-            in_=x_scales.rearrange("z q n -> q z n").bitcast(I32),
-        )
+        nc.vector.memset(xs[:].bitcast(I32), 0)
         nc.sync.dma_start(offs_t[:], offs)
+        for z in range(PASSES):
+            nc.sync.dma_start(
+                out=w1_raw[z][:], in_=w1[512 * z : 512 * (z + 1), :].rearrange("(p j) c -> p j c", j=PACK)
+            )
+            if z == 0:
+                nc.sync.dma_start(
+                    out=xs[0:P:8, :].bitcast(I32).rearrange("q (z n) -> q z n", z=PASSES),
+                    in_=x_scales.rearrange("z q n -> q z n").bitcast(I32),
+                )
+        for z in range(PASSES):
+            nc.sync.dma_start(
+                out=xw[z][:].bitcast(I32), in_=x_words[z].rearrange("p n t -> p (n t)").bitcast(I32)
+            )
         nc.sync.dma_start(cell_t[:], cell)
         nc.sync.dma_start(pos_t[0][:], pos1)
         nc.sync.dma_start(pos_t[1][:], pos2)
-        nc.sync.dma_start(out=w1_raw[0][:, 2:4, :], in_=w1_v[0][:, 2:4, :])
-        x_v = [x_words[z].rearrange("p n t -> p (n t)").bitcast(I32) for z in range(PASSES)]
-        nc.sync.dma_start(out=xw[0][:].bitcast(I32), in_=x_v[0])
-        nc.sync.dma_start(out=w1_raw[1][:], in_=w1_v[1])
 
-        xs_at = sb("xs_at", [P, PASSES * S], U8)
-        nc.vector.memset(xs_at[:].bitcast(I32), 0)
-        nc.vector.memset(win[0][:], 0.0)
-        for n in (1, 2):
-            nc.gpsimd.memset(win[n][:], 0.0)
+        for n in range(3):
+            nc.vector.memset(win[n][:], 0.0)
 
         w1c = [[None, None] for z in range(PASSES)]
         w1s = [[None, None] for z in range(PASSES)]
@@ -78,10 +77,10 @@ def tile_picked_devox_none_p_kernel(
             nc.vector.tensor_copy(
                 out=xs_g[:, z * S : (z + 1) * S], in_=xs[:, z * T : (z + 1) * T].indirect(offs_t[:])
             )
-        for r in range(4):
-            nc.sync.dma_start(out=xs_at[r:P:32, :].bitcast(I32), in_=xs_g[8 * r : P : 32, :].bitcast(I32))
-        xw.append(sb("xw1", [P, T], U32))
-        nc.sync.dma_start(out=xw[1][:].bitcast(I32), in_=x_v[1])
+        xs_at = sb("xs_at", [P, PASSES * S], U8)
+        nc.vector.tensor_copy(out=xs_at[:].bitcast(I32), in_=xs_g[:].bitcast(I32))
+        for r in range(1, 4):
+            nc.scalar.dma_start(out=xs_at[r:P:32, :].bitcast(I32), in_=xs_g[8 * r : P : 32, :].bitcast(I32))
         for z in range(PASSES):
             src = w1_raw[z][:].rearrange("p j (m t) -> p m j t", t=PACK)
             grouped = [sb("w1g%d_%d" % (z, u), [P, 2 * P * PACK], BF16) for u in range(2)]
@@ -95,9 +94,9 @@ def tile_picked_devox_none_p_kernel(
                 w1c[z][u] = sb("w1c%d_%d" % (z, u), [P, 2 * P], U32)
                 w1s[z][u] = sb("w1s%d_%d" % (z, u), [P, 2 * P], U8)
                 nc.vector.quantize_mx(out=w1c[z][u][:].bitcast(FP8X4), scales=w1s[z][u][:], in_=grouped[u][:])
-            if z == 0:
-                xg0 = sb("xg0", [P, S], U32)
-                nc.vector.tensor_copy(out=xg0[:], in_=xw[0][:].indirect(offs_t[:]))
+
+        xg0 = sb("xg0", [P, S], U32)
+        nc.vector.tensor_copy(out=xg0[:], in_=xw[0][:].indirect(offs_t[:]))
 
         xg1 = sb("xg1", [P, S], U32)
         for a in range(2):
@@ -147,10 +146,12 @@ def tile_picked_devox_none_p_kernel(
 
         pieces = [(1, 0, FIRST), (0, 0, FIRST), (1, FIRST, S), (0, FIRST, S), (3, 0, S), (2, 0, S)]
         accs = [bank(b) for b in range(len(pieces))]
-        for acc, (t, lo, hi) in zip(accs, pieces):
+        for acc, (t, lo, hi) in zip(accs[:4], pieces):
             first_product(acc, 0, t, lo, hi)
         hs = {}
         for acc, (t, lo, hi) in zip(accs, pieces):
+            if t >= 2:
+                first_product(acc, 0, t, lo, hi)
             first_product(acc, 1, t, lo, hi)
             hs[t] = rectify(t, acc[:, 0 : hi - lo], lo)
             if t < 2:

@@ -67,8 +67,9 @@ def tile_picked_devox_none_p_kernel(
         nc.sync.dma_start(pos_t[0][:], pos1)
         nc.sync.dma_start(pos_t[1][:], pos2)
 
-        for n in range(3):
-            nc.vector.memset(win[n][:], 0.0)
+        nc.vector.memset(win[0][:], 0.0)
+        for n in (1, 2):
+            nc.gpsimd.memset(win[n][:], 0.0)
 
         w1c = [[None, None] for z in range(PASSES)]
         w1s = [[None, None] for z in range(PASSES)]
@@ -80,7 +81,7 @@ def tile_picked_devox_none_p_kernel(
         xs_at = sb("xs_at", [P, PASSES * S], U8)
         nc.vector.tensor_copy(out=xs_at[:].bitcast(I32), in_=xs_g[:].bitcast(I32))
         for r in range(1, 4):
-            nc.scalar.dma_start(out=xs_at[r:P:32, :].bitcast(I32), in_=xs_g[8 * r : P : 32, :].bitcast(I32))
+            nc.sync.dma_start(out=xs_at[r:P:32, :].bitcast(I32), in_=xs_g[8 * r : P : 32, :].bitcast(I32))
         for z in range(PASSES):
             src = w1_raw[z][:].rearrange("p j (m t) -> p m j t", t=PACK)
             grouped = [sb("w1g%d_%d" % (z, u), [P, 2 * P * PACK], BF16) for u in range(2)]
@@ -105,8 +106,8 @@ def tile_picked_devox_none_p_kernel(
             )
         xg = [xg0, xg1]
         emb_v = emb.rearrange("(p t) r -> p t r", t=PACK)
-        emb_t = [sb("emb_t%d" % t, [P, U], F32, ("xw1", "xw0", "w1_raw1")[t]) for t in range(3)]
-        for t in (1, 0, 2):
+        emb_t = [sb("emb_t%d" % t, [P, U], F32, ("xw1", "xw0", "w1g1_0", "w1_raw1")[t]) for t in range(4)]
+        for t in (1, 0, 3, 2):
             nc.sync.dma_start(out=emb_t[t][:], in_=emb_v[:, t, :])
 
         def first_product(acc, z, t, lo, hi):
@@ -138,28 +139,31 @@ def tile_picked_devox_none_p_kernel(
             words = pairs[c][:, u * CHUNK : (u + 1) * CHUNK]
             return words.bitcast(BF16).rearrange("p (r e) -> p r e", e=2)[:, :, e]
 
-        def add_plane(t):
-            for c in ORDER:
-                cols = slice(c * CHUNK, (c + 1) * CHUNK)
-                other = pairs[c][:, CHUNK:] if t == 3 else emb_t[t][:, cols]
-                nc.gpsimd.tensor_tensor(out=halves(c, t), in0=up[t][:, cols], in1=other, op=ADD)
+        low = sb("low", [P, 2, U], BF16)
+
+        third = sb("third", [P, U], BF16)
+
+        def add(dst, t, parts):
+            for lo, hi in parts:
+                cols = slice(lo * CHUNK, hi * CHUNK)
+                nc.gpsimd.tensor_tensor(out=dst[:, cols], in0=up[t][:, cols], in1=emb_t[t][:, cols], op=ADD)
+
+        def pair(c, u, src):
+            nc.scalar.copy(
+                out=pairs[c][:, u * CHUNK : (u + 1) * CHUNK].bitcast(BF16).rearrange("p (r e) -> p r e", e=2), in_=src
+            )
 
         pieces = [(1, 0, FIRST), (0, 0, FIRST), (1, FIRST, S), (0, FIRST, S), (3, 0, S), (2, 0, S)]
         accs = [bank(b) for b in range(len(pieces))]
-        for acc, (t, lo, hi) in zip(accs[:4], pieces):
-            first_product(acc, 0, t, lo, hi)
         hs = {}
         for acc, (t, lo, hi) in zip(accs, pieces):
-            if t >= 2:
-                first_product(acc, 0, t, lo, hi)
+            first_product(acc, 0, t, lo, hi)
             first_product(acc, 1, t, lo, hi)
             hs[t] = rectify(t, acc[:, 0 : hi - lo], lo)
             if t < 2:
                 place(t, hs[t], lo, hi)
 
-        pairs = [sb("pairs%d" % c, [P, 2 * CHUNK], F32, "w1c%d_%d" % divmod(c, 2)) for c in range(nchunk)]
-        for c in range(nchunk):
-            nc.sync.dma_start(out=pairs[c][:, CHUNK:], in_=emb_v[:, 3, c * CHUNK : (c + 1) * CHUNK])
+        pairs = [sb("pairs%d" % c, [P, 2 * CHUNK], F32) for c in range(nchunk)]
         w2w = sb("w2w", [P, N], U32, "xg1")
         nc.sync.dma_start(out=w2w[:].bitcast(I32), in_=w2_words[0].rearrange("p n t -> p (n t)").bitcast(I32))
         w2s = sb("w2s", [P, N], U8, "w1s0_0")
@@ -172,15 +176,18 @@ def tile_picked_devox_none_p_kernel(
         gate_t = sb("gate_t", [P, 2, V], F32, "xg0")
         nc.sync.dma_start(out=gate_t[:], in_=gate.rearrange("d p v -> p d v"))
 
-        add_plane(1)
-        add_plane(0)
-        for t in (3, 2):
-            place(t, hs[t], 0, S)
-            if t != 2:
-                add_plane(t)
+        add(low[:, 1, :], 1, [(0, 4)])
+        add(low[:, 0, :], 0, [(0, 2), (2, 4)])
+        for c in ORDER:
+            pair(c, 0, low[:, :, c * CHUNK : (c + 1) * CHUNK].rearrange("p e r -> p r e"))
+        place(3, hs[3], 0, S)
+        add(third[:], 3, [(0, 2), (3, 4), (2, 3)])
+        for c in ORDER:
+            pair(c, 1, third[:, c * CHUNK : (c + 1) * CHUNK].unsqueeze(2).to_broadcast([P, CHUNK, 2]))
+        place(2, hs[2], 0, S)
 
-        def quantise(name, src, width):
-            codes = sb("c" + name, [P, width], U32)
+        def quantise(name, src, width, tag=None):
+            codes = sb("c" + name, [P, width], U32, tag)
             scales = sb("s" + name, [P, width], U8)
             nc.vector.quantize_mx(out=codes[:].bitcast(FP8X4), scales=scales[:], in_=src)
             return codes, scales
@@ -192,7 +199,7 @@ def tile_picked_devox_none_p_kernel(
         for c in ORDER:
             nc.vector.tensor_tensor(out=halves(c, 2), in0=up[2][:, chunks[c]], in1=emb_t[2][:, chunks[c]], op=ADD)
         for c in range(nchunk):
-            zq[c] = sb("zi%d" % c, [P, CHUNK * PACK], BF16)
+            zq[c] = sb("zi%d" % c, [P, CHUNK * PACK], BF16, {0: "third", 3: "w1g1_0"}.get(c))
             words = pairs[c][:].rearrange("p (u r) -> p r u", u=2)
             weave = nc.vector.tensor_copy if c == 3 else nc.scalar.copy
             weave(out=zq[c][:].bitcast(F32).rearrange("p (r u) -> p r u", u=2), in_=words)
@@ -211,7 +218,7 @@ def tile_picked_devox_none_p_kernel(
             leave(out=y[:, at + lo : at + hi], in_=acc[:, 0 : hi - lo])
 
         for c in ORDER:
-            zc, zs = quantise("z%d" % c, zq[c][:], CHUNK)
+            zc, zs = quantise("z%d" % c, zq[c][:], CHUNK, "win0" if c == 0 else None)
             if c == ORDER[-1]:
                 second_product(1, zc, zs, c * CHUNK, 0, CHUNK // 2, nc.scalar.copy)
                 second_product(2, zc, zs, c * CHUNK, CHUNK // 2, CHUNK, nc.vector.tensor_copy)

@@ -22,7 +22,6 @@ PASSES = 2
 HALF = S // 2
 CHUNK = 256
 FIRST = 128
-ORDER = (0, 1, 3, 2)
 
 
 def tile_picked_devox_none_p_kernel(
@@ -49,7 +48,6 @@ def tile_picked_devox_none_p_kernel(
         up = [win[1], win[0], win[0], win[2]]
 
         nc.vector.memset(xs[:].bitcast(I32), 0)
-        nc.sync.dma_start(offs_t[:], offs)
         for z in range(PASSES):
             nc.sync.dma_start(
                 out=w1_raw[z][:], in_=w1[512 * z : 512 * (z + 1), :].rearrange("(p j) c -> p j c", j=PACK)
@@ -59,6 +57,7 @@ def tile_picked_devox_none_p_kernel(
                     out=xs[0:P:8, :].bitcast(I32).rearrange("q (z n) -> q z n", z=PASSES),
                     in_=x_scales.rearrange("z q n -> q z n").bitcast(I32),
                 )
+                nc.sync.dma_start(offs_t[:], offs)
         for z in range(PASSES):
             nc.sync.dma_start(
                 out=xw[z][:].bitcast(I32), in_=x_words[z].rearrange("p n t -> p (n t)").bitcast(I32)
@@ -88,7 +87,7 @@ def tile_picked_devox_none_p_kernel(
             nc.scalar.copy(
                 out=grouped[1][:].rearrange("p (t m j) -> p m j t", t=2, j=PACK), in_=src[:, :, :, 2:4]
             )
-            nc.vector.tensor_copy(
+            (nc.scalar.copy if z == 0 else nc.vector.tensor_copy)(
                 out=grouped[0][:].rearrange("p (t m j) -> p m j t", t=2, j=PACK), in_=src[:, :, :, 0:2]
             )
             for u in range(2):
@@ -106,8 +105,8 @@ def tile_picked_devox_none_p_kernel(
             )
         xg = [xg0, xg1]
         emb_v = emb.rearrange("(p t) r -> p t r", t=PACK)
-        emb_t = [sb("emb_t%d" % t, [P, U], F32, ("xw1", "xw0", "w1g1_0", "w1_raw1")[t]) for t in range(4)]
-        for t in (1, 0, 3, 2):
+        emb_t = [sb("emb_t%d" % t, [P, U], F32, ("xw1", "xw0", "w1g1_0")[t]) for t in range(3)]
+        for t in (1, 0, 2):
             nc.sync.dma_start(out=emb_t[t][:], in_=emb_v[:, t, :])
 
         def first_product(acc, z, t, lo, hi):
@@ -134,24 +133,10 @@ def tile_picked_devox_none_p_kernel(
 
         nchunk = U // CHUNK
 
-        def halves(c, t):
+        def halves(t, cols):
             u, e = divmod(t, 2)
-            words = pairs[c][:, u * CHUNK : (u + 1) * CHUNK]
+            words = pairs[:, u * U + cols.start : u * U + cols.stop]
             return words.bitcast(BF16).rearrange("p (r e) -> p r e", e=2)[:, :, e]
-
-        low = sb("low", [P, 2, U], BF16)
-
-        third = sb("third", [P, U], BF16)
-
-        def add(dst, t, parts):
-            for lo, hi in parts:
-                cols = slice(lo * CHUNK, hi * CHUNK)
-                nc.gpsimd.tensor_tensor(out=dst[:, cols], in0=up[t][:, cols], in1=emb_t[t][:, cols], op=ADD)
-
-        def pair(c, u, src):
-            nc.scalar.copy(
-                out=pairs[c][:, u * CHUNK : (u + 1) * CHUNK].bitcast(BF16).rearrange("p (r e) -> p r e", e=2), in_=src
-            )
 
         pieces = [(1, 0, FIRST), (0, 0, FIRST), (1, FIRST, S), (0, FIRST, S), (3, 0, S), (2, 0, S)]
         accs = [bank(b) for b in range(len(pieces))]
@@ -163,7 +148,8 @@ def tile_picked_devox_none_p_kernel(
             if t < 2:
                 place(t, hs[t], lo, hi)
 
-        pairs = [sb("pairs%d" % c, [P, 2 * CHUNK], F32) for c in range(nchunk)]
+        pairs = sb("pairs", [P, 2 * U], F32, "w1_raw1")
+        nc.sync.dma_start(out=pairs[:, U:], in_=emb_v[:, 3, :])
         w2w = sb("w2w", [P, N], U32, "xg1")
         nc.sync.dma_start(out=w2w[:].bitcast(I32), in_=w2_words[0].rearrange("p n t -> p (n t)").bitcast(I32))
         w2s = sb("w2s", [P, N], U8, "w1s0_0")
@@ -176,14 +162,11 @@ def tile_picked_devox_none_p_kernel(
         gate_t = sb("gate_t", [P, 2, V], F32, "xg0")
         nc.sync.dma_start(out=gate_t[:], in_=gate.rearrange("d p v -> p d v"))
 
-        add(low[:, 1, :], 1, [(0, 4)])
-        add(low[:, 0, :], 0, [(0, 2), (2, 4)])
-        for c in ORDER:
-            pair(c, 0, low[:, :, c * CHUNK : (c + 1) * CHUNK].rearrange("p e r -> p r e"))
+        cells = slice(0, U)
+        for t in (1, 0):
+            nc.gpsimd.tensor_tensor(out=halves(t, cells), in0=up[t][:], in1=emb_t[t][:], op=ADD)
         place(3, hs[3], 0, S)
-        add(third[:], 3, [(0, 2), (3, 4), (2, 3)])
-        for c in ORDER:
-            pair(c, 1, third[:, c * CHUNK : (c + 1) * CHUNK].unsqueeze(2).to_broadcast([P, CHUNK, 2]))
+        nc.gpsimd.tensor_tensor(out=halves(3, cells), in0=up[3][:], in1=pairs[:, U:], op=ADD)
         place(2, hs[2], 0, S)
 
         def quantise(name, src, width, tag=None):
@@ -195,14 +178,16 @@ def tile_picked_devox_none_p_kernel(
         y = sb("y", [P, U], F32)
         edges = (0, 256, 512, 768, 1024)
         chunks = [slice(lo, hi) for lo, hi in zip(edges, edges[1:])]
-        zq = {}
-        for c in ORDER:
-            nc.vector.tensor_tensor(out=halves(c, 2), in0=up[2][:, chunks[c]], in1=emb_t[2][:, chunks[c]], op=ADD)
-        for c in range(nchunk):
-            zq[c] = sb("zi%d" % c, [P, CHUNK * PACK], BF16, {0: "third", 3: "w1g1_0"}.get(c))
-            words = pairs[c][:].rearrange("p (u r) -> p r u", u=2)
-            weave = nc.vector.tensor_copy if c == 3 else nc.scalar.copy
-            weave(out=zq[c][:].bitcast(F32).rearrange("p (r u) -> p r u", u=2), in_=words)
+        for cols in chunks:
+            nc.vector.tensor_tensor(out=halves(2, cols), in0=up[2][:, cols], in1=emb_t[2][:, cols], op=ADD)
+        zq = []
+        for c, cols in enumerate(chunks):
+            zq.append(sb("zi%d" % c, [P, CHUNK * PACK], BF16))
+            weave = nc.vector.tensor_copy if c == 2 else nc.scalar.copy
+            weave(
+                out=zq[c][:].bitcast(F32).rearrange("p (r u) -> p r u", u=2),
+                in_=pairs[:].rearrange("p (u r) -> p r u", u=2)[:, cols],
+            )
 
         def second_product(b, zc, zs, at, lo, hi, leave):
             acc = bank(b)
@@ -217,13 +202,13 @@ def tile_picked_devox_none_p_kernel(
             )
             leave(out=y[:, at + lo : at + hi], in_=acc[:, 0 : hi - lo])
 
-        for c in ORDER:
-            zc, zs = quantise("z%d" % c, zq[c][:], CHUNK, "win0" if c == 0 else None)
-            if c == ORDER[-1]:
+        for c in range(nchunk):
+            zc, zs = quantise("z%d" % c, zq[c][:], CHUNK)
+            if c == nchunk - 1:
                 second_product(1, zc, zs, c * CHUNK, 0, CHUNK // 2, nc.scalar.copy)
                 second_product(2, zc, zs, c * CHUNK, CHUNK // 2, CHUNK, nc.vector.tensor_copy)
             else:
-                second_product((6, 7, None, 0)[c], zc, zs, c * CHUNK, 0, CHUNK, nc.scalar.copy)
+                second_product((6, 7, 0)[c], zc, zs, c * CHUNK, 0, CHUNK, nc.scalar.copy)
 
         spans = [(0, 384), (384, 512)]
         g = [[sb("g%d_%d" % (a, d), [P, hi - lo], F32) for d in range(2)] for a, (lo, hi) in enumerate(spans)]

@@ -66,9 +66,8 @@ def tile_picked_devox_none_p_kernel(
         nc.sync.dma_start(pos_t[0][:], pos1)
         nc.sync.dma_start(pos_t[1][:], pos2)
 
-        nc.vector.memset(win[0][:], 0.0)
-        for n in (1, 2):
-            nc.gpsimd.memset(win[n][:], 0.0)
+        for n in range(3):
+            nc.vector.memset(win[n][:], 0.0)
 
         w1c = [[None, None] for z in range(PASSES)]
         w1s = [[None, None] for z in range(PASSES)]

@@ -15,13 +15,13 @@ FP8X4 = mybir.dt.float8_e4m3fn_x4
 ADD = mybir.AluOpType.add
 MULT = mybir.AluOpType.mult
 RELU = mybir.ActivationFunctionType.Relu
+COPY = mybir.ActivationFunctionType.Copy
 
 P = 128
 PACK = 4
 PASSES = 2
-HALF = S // 2
+LINE = 4
 CHUNK = 256
-FIRST = 128
 
 
 def tile_picked_devox_none_p_kernel(
@@ -38,14 +38,16 @@ def tile_picked_devox_none_p_kernel(
         def bank(b):
             return psum.tile([P, 512], F32, name="bank%d" % b, tag="bank%d" % b)
 
+        def entries(lst, lo, hi):
+            return lst[:, lo // 16 : hi // 16]
+
         offs_t = sb("offs_t", [P, S // 16], U16)
         cell_t = sb("cell_t", [P, S // 16], U16)
         pos_t = [sb("pos_t%d" % d, [P, V // 16], U16) for d in range(2)]
         xs = sb("xs", [P, PASSES * T], U8)
         w1_raw = [sb("w1_raw%d" % z, [P, PACK, H], F32) for z in range(PASSES)]
         xw = [sb("xw%d" % z, [P, T], U32) for z in range(PASSES)]
-        win = [sb("win%d" % n, [P, U], F32) for n in range(3)]
-        up = [win[1], win[0], win[0], win[2]]
+        win = [sb("win%d" % t, [P, U], F32) for t in range(2)]
 
         nc.vector.memset(xs[:].bitcast(I32), 0)
         for z in range(PASSES):
@@ -66,11 +68,9 @@ def tile_picked_devox_none_p_kernel(
         nc.sync.dma_start(pos_t[0][:], pos1)
         nc.sync.dma_start(pos_t[1][:], pos2)
 
-        for n in range(3):
-            nc.vector.memset(win[n][:], 0.0)
+        for t in range(2):
+            nc.vector.memset(win[t][:], 0.0)
 
-        w1c = [[None, None] for z in range(PASSES)]
-        w1s = [[None, None] for z in range(PASSES)]
         xs_g = sb("xs_g", [P, PASSES * S], U8)
         for z in range(PASSES):
             nc.vector.tensor_copy(
@@ -80,76 +80,93 @@ def tile_picked_devox_none_p_kernel(
         nc.vector.tensor_copy(out=xs_at[:].bitcast(I32), in_=xs_g[:].bitcast(I32))
         for r in range(1, 4):
             nc.sync.dma_start(out=xs_at[r:P:32, :].bitcast(I32), in_=xs_g[8 * r : P : 32, :].bitcast(I32))
+
+        w1c = [[None, None] for z in range(PASSES)]
+        w1s = [[None, None] for z in range(PASSES)]
         for z in range(PASSES):
             src = w1_raw[z][:].rearrange("p j (m t) -> p m j t", t=PACK)
             grouped = [sb("w1g%d_%d" % (z, u), [P, 2 * P * PACK], BF16) for u in range(2)]
             nc.scalar.copy(
-                out=grouped[1][:].rearrange("p (t m j) -> p m j t", t=2, j=PACK), in_=src[:, :, :, 2:4]
+                out=grouped[0][:].rearrange("p (t m j) -> p m j t", t=2, j=PACK), in_=src[:, :, :, 0:2]
             )
             (nc.scalar.copy if z == 0 else nc.vector.tensor_copy)(
-                out=grouped[0][:].rearrange("p (t m j) -> p m j t", t=2, j=PACK), in_=src[:, :, :, 0:2]
+                out=grouped[1][:].rearrange("p (t m j) -> p m j t", t=2, j=PACK), in_=src[:, :, :, 2:4]
             )
             for u in range(2):
                 w1c[z][u] = sb("w1c%d_%d" % (z, u), [P, 2 * P], U32)
                 w1s[z][u] = sb("w1s%d_%d" % (z, u), [P, 2 * P], U8)
                 nc.vector.quantize_mx(out=w1c[z][u][:].bitcast(FP8X4), scales=w1s[z][u][:], in_=grouped[u][:])
 
-        xg0 = sb("xg0", [P, S], U32)
-        nc.vector.tensor_copy(out=xg0[:], in_=xw[0][:].indirect(offs_t[:]))
+        xg = [sb("xg%d" % z, [P, S], U32) for z in range(PASSES)]
+        nc.vector.tensor_copy(out=xg[0][:], in_=xw[0][:].indirect(offs_t[:]))
+        for lo, hi in ((0, 128), (128, 256), (256, 512)):
+            nc.vector.tensor_copy(out=xg[1][:, lo:hi], in_=xw[1][:].indirect(entries(offs_t, lo, hi)))
 
-        xg1 = sb("xg1", [P, S], U32)
-        for a in range(2):
-            nc.vector.tensor_copy(
-                out=xg1[:, a * HALF : (a + 1) * HALF], in_=xw[1][:].indirect(offs_t[:, 16 * a : 16 * (a + 1)])
-            )
-        xg = [xg0, xg1]
         emb_v = emb.rearrange("(p t) r -> p t r", t=PACK)
-        emb_t = [sb("emb_t%d" % t, [P, U], F32, ("xw1", "xw0", "w1g1_0")[t]) for t in range(3)]
-        for t in (1, 0, 2):
-            nc.sync.dma_start(out=emb_t[t][:], in_=emb_v[:, t, :])
+        emb1 = sb("emb1", [P, U], F32, "w1g1_1")
+        nc.sync.dma_start(out=emb1[:], in_=emb_v[:, 1, :])
+        wide3 = sb("wide3", [P, 2 * U], F32, "xw0")
+        nc.gpsimd.memset(wide3[:, 0:U], 0.0)
+        nc.sync.dma_start(out=wide3[:, U:], in_=emb_v[:, 2, :])
+        wide2 = sb("wide2", [P, 2 * U], F32, "xw1")
+        nc.gpsimd.memset(wide2[:, 0:U], 0.0)
+        nc.sync.dma_start(out=wide2[:, U:], in_=emb_v[:, 3, :])
+        up = [win[0], win[1], wide2, wide3]
 
-        def first_product(acc, z, t, lo, hi):
+        def first_product(acc, t, lo, hi):
             u, e = divmod(t, 2)
-            cuts = [lo, HALF, hi] if lo == FIRST else [lo, hi]
-            for a, b in zip(cuts, cuts[1:]):
-                nc.tensor.matmul_mx(
-                    out=acc[:, a - lo : b - lo],
-                    lhsT=w1c[z][u][:, e * P : (e + 1) * P].bitcast(FP8X4),
-                    lhsT_scale=w1s[z][u][:, e * P : (e + 1) * P],
-                    rhs=xg[z][:, a:b].bitcast(FP8X4),
-                    rhs_scale=xs_at[:, z * S + a : z * S + b],
-                    start=(z == 0 and a == lo),
-                    stop=(z == PASSES - 1 and b == hi),
-                )
+            cuts = [lo, 256, hi] if lo == 128 else [lo, hi]
+            for z in range(PASSES):
+                for a, b in zip(cuts, cuts[1:]):
+                    nc.tensor.matmul_mx(
+                        out=acc[:, a - lo : b - lo],
+                        lhsT=w1c[z][u][:, e * P : (e + 1) * P].bitcast(FP8X4),
+                        lhsT_scale=w1s[z][u][:, e * P : (e + 1) * P],
+                        rhs=xg[z][:, a:b].bitcast(FP8X4),
+                        rhs_scale=xs_at[:, z * S + a : z * S + b],
+                        start=(z == 0 and a == lo),
+                        stop=(z == PASSES - 1 and b == hi),
+                    )
 
-        def rectify(t, src, lo):
-            h = sb("h%d_%d" % (t, lo), [P, src.shape[1]], F32)
-            nc.scalar.activation(out=h[:], in_=src, func=RELU)
+        def rectify(t, lo, hi, b, on_scalar, h=None):
+            acc = bank(b)
+            first_product(acc, t, lo, hi)
+            if h is None:
+                h = sb("h%d_%d" % (t, lo), [P, hi - lo], F32)[:]
+            if on_scalar:
+                nc.scalar.activation(out=h, in_=acc[:, 0 : hi - lo], func=RELU)
+            else:
+                nc.vector.tensor_scalar_max(out=h, in0=acc[:, 0 : hi - lo], scalar1=0.0)
             return h
 
         def place(t, h, lo, hi):
-            nc.vector.tensor_copy(out=up[t][:].indirect(cell_t[:, lo // 16 : hi // 16]), in_=h[:])
+            target = up[t][:].indirect(entries(cell_t, lo, hi))
+            if t % 2:
+                nc.scalar.activation(out=target, in_=h, func=COPY)
+            else:
+                nc.vector.tensor_copy(out=target, in_=h)
 
-        nchunk = U // CHUNK
+        h10 = rectify(1, 0, 128, 0, True)
+        place(1, h10, 0, 128)
+        h00 = rectify(0, 0, 256, 1, False)
+        place(0, h00, 0, 256)
+        h11 = rectify(1, 128, 512, 2, True)
+        h30 = rectify(3, 0, 256, 3, True)
+        place(1, h11, 128, 512)
+        h01 = rectify(0, 256, 512, 4, False)
+        h20 = rectify(2, 0, 256, 5, False)
+        place(0, h01, 256, 512)
+        h31 = rectify(3, 256, 512, 6, True)
+        place(3, h30, 0, 256)
+        place(2, h20, 0, 256)
+        pairs = sb("pairs", [P, 2 * U], F32, "w1c1_0")
+        nc.sync.dma_start(out=pairs[:, U:], in_=emb_v[:, 0, :])
+        h21 = rectify(2, 256, 512, 7, True, pairs[:, 0:CHUNK])
+        place(3, h31, 256, 512)
+        place(2, h21, 256, 512)
 
-        def halves(t, cols):
-            u, e = divmod(t, 2)
-            words = pairs[:, u * U + cols.start : u * U + cols.stop]
-            return words.bitcast(BF16).rearrange("p (r e) -> p r e", e=2)[:, :, e]
-
-        pieces = [(1, 0, FIRST), (0, 0, FIRST), (1, FIRST, S), (0, FIRST, S), (3, 0, S), (2, 0, S)]
-        accs = [bank(b) for b in range(len(pieces))]
-        hs = {}
-        for acc, (t, lo, hi) in zip(accs, pieces):
-            first_product(acc, 0, t, lo, hi)
-            first_product(acc, 1, t, lo, hi)
-            hs[t] = rectify(t, acc[:, 0 : hi - lo], lo)
-            if t < 2:
-                place(t, hs[t], lo, hi)
-
-        pairs = sb("pairs", [P, 2 * U], F32, "w1_raw1")
-        nc.sync.dma_start(out=pairs[:, U:], in_=emb_v[:, 3, :])
-        w2w = sb("w2w", [P, N], U32, "xg1")
+        embs = [pairs[:, U:], emb1[:]]
+        w2w = sb("w2w", [P, N], U32, "xg0")
         nc.sync.dma_start(out=w2w[:].bitcast(I32), in_=w2_words[0].rearrange("p n t -> p (n t)").bitcast(I32))
         w2s = sb("w2s", [P, N], U8, "w1s0_0")
         nc.gpsimd.memset(w2s[:].bitcast(I32), 0)
@@ -158,35 +175,39 @@ def tile_picked_devox_none_p_kernel(
                 out=w2s[32 * q : 32 * q + 4, :].bitcast(I32),
                 in_=w2_scales[0, 4 * q : 4 * q + 4, :].bitcast(I32),
             )
-        gate_t = sb("gate_t", [P, 2, V], F32, "xg0")
+        gate_t = sb("gate_t", [P, 2, V], F32, "w1c0_1")
         nc.sync.dma_start(out=gate_t[:], in_=gate.rearrange("d p v -> p d v"))
 
-        cells = slice(0, U)
-        for t in (1, 0):
-            nc.gpsimd.tensor_tensor(out=halves(t, cells), in0=up[t][:], in1=emb_t[t][:], op=ADD)
-        place(3, hs[3], 0, S)
-        nc.gpsimd.tensor_tensor(out=halves(3, cells), in0=up[3][:], in1=pairs[:, U:], op=ADD)
-        place(2, hs[2], 0, S)
+        def words(u, lo, hi):
+            return pairs[:, u * U + lo : u * U + hi]
 
-        def quantise(name, src, width, tag=None):
-            codes = sb("c" + name, [P, width], U32, tag)
-            scales = sb("s" + name, [P, width], U8)
-            nc.vector.quantize_mx(out=codes[:].bitcast(FP8X4), scales=scales[:], in_=src)
-            return codes, scales
+        def add_low(engine, t, lo, hi):
+            half = words(0, lo, hi).bitcast(BF16).rearrange("p (r e) -> p r e", e=2)[:, :, t]
+            engine.tensor_tensor(out=half, in0=up[t][:, lo:hi], in1=embs[t][:, lo:hi], op=ADD)
+
+        def add_high(lo, hi):
+            lines = slice(lo // LINE, hi // LINE)
+            a = wide2[:].rearrange("p (e c i) -> p c e i", e=2, i=LINE)[:, lines]
+            b = wide3[:].rearrange("p (e c i) -> p c e i", e=2, i=LINE)[:, lines, ::-1, :]
+            both = words(1, lo, hi).bitcast(BF16).rearrange("p (c i e) -> p c e i", e=2, i=LINE)
+            nc.vector.tensor_tensor(out=both, in0=a, in1=b, op=ADD)
+
+        for t in (1, 0):
+            add_low(nc.gpsimd, t, CHUNK, U)
+        for t in range(2):
+            add_low(nc.vector, t, 0, CHUNK)
+
+        nchunk = U // CHUNK
+        zq = [sb("zi%d" % c, [P, CHUNK * PACK], BF16) for c in range(nchunk)]
+
+        def weave(c):
+            add_high(c * CHUNK, (c + 1) * CHUNK)
+            (nc.vector.tensor_copy if c == nchunk - 1 else nc.scalar.copy)(
+                out=zq[c][:].bitcast(F32).rearrange("p (r u) -> p r u", u=2),
+                in_=pairs[:].rearrange("p (u r) -> p r u", u=2)[:, c * CHUNK : (c + 1) * CHUNK],
+            )
 
         y = sb("y", [P, U], F32)
-        edges = (0, 256, 512, 768, 1024)
-        chunks = [slice(lo, hi) for lo, hi in zip(edges, edges[1:])]
-        for cols in chunks:
-            nc.vector.tensor_tensor(out=halves(2, cols), in0=up[2][:, cols], in1=emb_t[2][:, cols], op=ADD)
-        zq = []
-        for c, cols in enumerate(chunks):
-            zq.append(sb("zi%d" % c, [P, CHUNK * PACK], BF16))
-            weave = nc.vector.tensor_copy if c == 2 else nc.scalar.copy
-            weave(
-                out=zq[c][:].bitcast(F32).rearrange("p (r u) -> p r u", u=2),
-                in_=pairs[:].rearrange("p (u r) -> p r u", u=2)[:, cols],
-            )
 
         def second_product(b, zc, zs, at, lo, hi, leave):
             acc = bank(b)
@@ -201,25 +222,30 @@ def tile_picked_devox_none_p_kernel(
             )
             leave(out=y[:, at + lo : at + hi], in_=acc[:, 0 : hi - lo])
 
+        weave(0)
         for c in range(nchunk):
-            zc, zs = quantise("z%d" % c, zq[c][:], CHUNK)
+            if c + 1 < nchunk:
+                weave(c + 1)
+            zc = sb("zc%d" % c, [P, CHUNK], U32, "win0" if c == 0 else None)
+            zs = sb("zs%d" % c, [P, CHUNK], U8)
+            nc.vector.quantize_mx(out=zc[:].bitcast(FP8X4), scales=zs[:], in_=zq[c][:])
             if c == nchunk - 1:
-                second_product(1, zc, zs, c * CHUNK, 0, CHUNK // 2, nc.scalar.copy)
-                second_product(2, zc, zs, c * CHUNK, CHUNK // 2, CHUNK, nc.vector.tensor_copy)
+                second_product(3, zc, zs, c * CHUNK, 0, CHUNK // 2, nc.scalar.copy)
+                second_product(4, zc, zs, c * CHUNK, CHUNK // 2, CHUNK, nc.vector.tensor_copy)
             else:
-                second_product((6, 7, 0)[c], zc, zs, c * CHUNK, 0, CHUNK, nc.scalar.copy)
+                second_product(c, zc, zs, c * CHUNK, 0, CHUNK, nc.scalar.copy)
 
-        spans = [(0, 384), (384, 512)]
-        g = [[sb("g%d_%d" % (a, d), [P, hi - lo], F32) for d in range(2)] for a, (lo, hi) in enumerate(spans)]
+        parts = [(0, 384), (384, 512)]
+        g = [[sb("g%d_%d" % (a, d), [P, hi - lo], F32) for d in range(2)] for a, (lo, hi) in enumerate(parts)]
 
         def fetch(a, d):
-            lo, hi = spans[a]
+            lo, hi = parts[a]
             nc.vector.tensor_tensor(
-                out=g[a][d][:], in0=y[:].indirect(pos_t[d][:, lo // 16 : hi // 16]), in1=gate_t[:, d, lo:hi], op=MULT
+                out=g[a][d][:], in0=y[:].indirect(entries(pos_t[d], lo, hi)), in1=gate_t[:, d, lo:hi], op=MULT
             )
 
         def finish(a):
-            lo, hi = spans[a]
+            lo, hi = parts[a]
             o = sb("o%d" % a, [P, hi - lo], F32)
             nc.vector.tensor_tensor(out=o[:], in0=g[a][0][:], in1=g[a][1][:], op=ADD)
             nc.sync.dma_start(out=out[:, lo:hi], in_=o[:])

@@ -21,7 +21,6 @@ P = 128
 PACK = 4
 PASSES = 2
 LINE = 4
-CHUNK = 256
 
 
 def tile_picked_devox_none_p_kernel(
@@ -128,11 +127,10 @@ def tile_picked_devox_none_p_kernel(
                         stop=(z == PASSES - 1 and b == hi),
                     )
 
-        def rectify(t, lo, hi, b, on_scalar, h=None):
+        def rectify(t, lo, hi, b, on_scalar):
             acc = bank(b)
             first_product(acc, t, lo, hi)
-            if h is None:
-                h = sb("h%d_%d" % (t, lo), [P, hi - lo], F32)[:]
+            h = sb("h%d_%d" % (t, lo), [P, hi - lo], F32)[:]
             if on_scalar:
                 nc.scalar.activation(out=h, in_=acc[:, 0 : hi - lo], func=RELU)
             else:
@@ -161,7 +159,7 @@ def tile_picked_devox_none_p_kernel(
         place(2, h20, 0, 256)
         pairs = sb("pairs", [P, 2 * U], F32, "w1c1_0")
         nc.sync.dma_start(out=pairs[:, U:], in_=emb_v[:, 0, :])
-        h21 = rectify(2, 256, 512, 7, True, pairs[:, 0:CHUNK])
+        h21 = rectify(2, 256, 512, 7, True)
         place(3, h31, 256, 512)
         place(2, h21, 256, 512)
 
@@ -193,66 +191,64 @@ def tile_picked_devox_none_p_kernel(
             nc.vector.tensor_tensor(out=both, in0=a, in1=b, op=ADD)
 
         for t in (1, 0):
-            add_low(nc.gpsimd, t, CHUNK, U)
-        for t in range(2):
-            add_low(nc.vector, t, 0, CHUNK)
+            add_low(nc.gpsimd, t, 0, U)
 
-        nchunk = U // CHUNK
-        zq = [sb("zi%d" % c, [P, CHUNK * PACK], BF16) for c in range(nchunk)]
+        edges = (0, 256, 512, 768, 896, 1024)
+        chunks = list(zip(edges, edges[1:]))
+        zq = [sb("zi%d" % c, [P, (hi - lo) * PACK], BF16) for c, (lo, hi) in enumerate(chunks)]
 
         def weave(c):
-            add_high(c * CHUNK, (c + 1) * CHUNK)
-            (nc.vector.tensor_copy if c == nchunk - 1 else nc.scalar.copy)(
+            lo, hi = chunks[c]
+            add_high(lo, hi)
+            nc.scalar.copy(
                 out=zq[c][:].bitcast(F32).rearrange("p (r u) -> p r u", u=2),
-                in_=pairs[:].rearrange("p (u r) -> p r u", u=2)[:, c * CHUNK : (c + 1) * CHUNK],
+                in_=pairs[:].rearrange("p (u r) -> p r u", u=2)[:, lo:hi],
             )
 
-        y = sb("y", [P, U], F32)
+        y = sb("y", [P, U], F32, "xw1")
 
-        def second_product(b, zc, zs, at, lo, hi, leave):
-            acc = bank(b)
+        def second_product(c, acc):
+            lo, hi = chunks[c]
+            zc = sb("zc%d" % c, [P, hi - lo], U32)
+            zs = sb("zs%d" % c, [P, hi - lo], U8)
+            nc.vector.quantize_mx(out=zc[:].bitcast(FP8X4), scales=zs[:], in_=zq[c][:])
             nc.tensor.matmul_mx(
-                out=acc[:, 0 : hi - lo],
+                out=acc,
                 lhsT=w2w[:].bitcast(FP8X4),
                 lhsT_scale=w2s[:],
-                rhs=zc[:, lo:hi].bitcast(FP8X4),
-                rhs_scale=zs[:, lo:hi],
+                rhs=zc[:].bitcast(FP8X4),
+                rhs_scale=zs[:],
                 start=True,
                 stop=True,
             )
-            leave(out=y[:, at + lo : at + hi], in_=acc[:, 0 : hi - lo])
 
+        accs = [bank(0), bank(1), bank(2)]
         weave(0)
-        for c in range(nchunk):
-            if c + 1 < nchunk:
-                weave(c + 1)
-            zc = sb("zc%d" % c, [P, CHUNK], U32, "win0" if c == 0 else None)
-            zs = sb("zs%d" % c, [P, CHUNK], U8)
-            nc.vector.quantize_mx(out=zc[:].bitcast(FP8X4), scales=zs[:], in_=zq[c][:])
-            if c == nchunk - 1:
-                second_product(3, zc, zs, c * CHUNK, 0, CHUNK // 2, nc.scalar.copy)
-                second_product(4, zc, zs, c * CHUNK, CHUNK // 2, CHUNK, nc.vector.tensor_copy)
-            else:
-                second_product(c, zc, zs, c * CHUNK, 0, CHUNK, nc.scalar.copy)
+        weave(1)
+        second_product(0, accs[0][:, 0:256])
+        weave(2)
+        second_product(1, accs[0][:, 256:512])
+        weave(3)
+        weave(4)
+        second_product(2, accs[1][:, 0:256])
+        nc.scalar.copy(out=y[:, 0:512], in_=accs[0][:])
+        second_product(3, accs[1][:, 256:384])
+        second_product(4, accs[2][:, 0:128])
+        nc.vector.tensor_copy(out=y[:, 512:896], in_=accs[1][:, 0:384])
+        nc.scalar.copy(out=y[:, 896:1024], in_=accs[2][:, 0:128])
 
         parts = [(0, 384), (384, 512)]
-        g = [[sb("g%d_%d" % (a, d), [P, hi - lo], F32) for d in range(2)] for a, (lo, hi) in enumerate(parts)]
-
-        def fetch(a, d):
-            lo, hi = parts[a]
+        first = [sb("first%d" % a, [P, hi - lo], F32) for a, (lo, hi) in enumerate(parts)]
+        second = [sb("second%d" % a, [P, hi - lo], F32) for a, (lo, hi) in enumerate(parts)]
+        for a, (lo, hi) in enumerate(parts):
+            nc.scalar.activation(out=second[a][:], in_=y[:].indirect(entries(pos_t[1], lo, hi)), func=COPY)
             nc.vector.tensor_tensor(
-                out=g[a][d][:], in0=y[:].indirect(entries(pos_t[d], lo, hi)), in1=gate_t[:, d, lo:hi], op=MULT
+                out=first[a][:], in0=y[:].indirect(entries(pos_t[0], lo, hi)), in1=gate_t[:, 0, lo:hi], op=MULT
             )
-
-        def finish(a):
-            lo, hi = parts[a]
+        weighted = [sb("weighted%d" % a, [P, hi - lo], F32) for a, (lo, hi) in enumerate(parts)]
+        for a, (lo, hi) in enumerate(parts):
+            nc.vector.tensor_tensor(out=weighted[a][:], in0=second[a][:], in1=gate_t[:, 1, lo:hi], op=MULT)
+        for a, (lo, hi) in enumerate(parts):
             o = sb("o%d" % a, [P, hi - lo], F32)
-            nc.vector.tensor_tensor(out=o[:], in0=g[a][0][:], in1=g[a][1][:], op=ADD)
+            nc.vector.tensor_tensor(out=o[:], in0=first[a][:], in1=weighted[a][:], op=ADD)
             nc.sync.dma_start(out=out[:, lo:hi], in_=o[:])
-
-        fetch(0, 0)
-        fetch(0, 1)
-        fetch(1, 0)
-        finish(0)
-        fetch(1, 1)
-        finish(1)

@@ -47,6 +47,8 @@ def tile_picked_devox_none_p_kernel(
         w1_raw = [sb("w1_raw%d" % z, [P, PACK, H], F32) for z in range(PASSES)]
         xw = [sb("xw%d" % z, [P, T], U32) for z in range(PASSES)]
         win = [sb("win%d" % t, [P, U], F32) for t in range(2)]
+        wide2 = sb("wide2", [P, 2 * U], F32)
+        wide3 = sb("wide3", [P, 2 * U], F32)
 
         nc.vector.memset(xs[:].bitcast(I32), 0)
         for z in range(PASSES):
@@ -67,8 +69,11 @@ def tile_picked_devox_none_p_kernel(
         nc.sync.dma_start(pos_t[0][:], pos1)
         nc.sync.dma_start(pos_t[1][:], pos2)
 
+        up = [win[0], win[1], wide2, wide3]
         for t in range(2):
             nc.vector.memset(win[t][:], 0.0)
+        for wide in (wide3, wide2):
+            nc.scalar.copy(out=wide[:, 0:U], in_=win[0][:])
 
         xs_g = sb("xs_g", [P, PASSES * S], U8)
         for z in range(PASSES):
@@ -84,17 +89,20 @@ def tile_picked_devox_none_p_kernel(
         w1s = [[None, None] for z in range(PASSES)]
         for z in range(PASSES):
             src = w1_raw[z][:].rearrange("p j (m t) -> p m j t", t=PACK)
-            grouped = [sb("w1g%d_%d" % (z, u), [P, 2 * P * PACK], BF16) for u in range(2)]
+            if z == 0:
+                grouped = [sb("w1g%d" % u, [P, 2 * P * PACK], BF16)[:] for u in range(2)]
+            else:
+                grouped = [wide[:, U : U + P * PACK].bitcast(BF16) for wide in (wide3, wide2)]
             nc.scalar.copy(
-                out=grouped[0][:].rearrange("p (t m j) -> p m j t", t=2, j=PACK), in_=src[:, :, :, 0:2]
+                out=grouped[0].rearrange("p (t m j) -> p m j t", t=2, j=PACK), in_=src[:, :, :, 0:2]
             )
             (nc.scalar.copy if z == 0 else nc.vector.tensor_copy)(
-                out=grouped[1][:].rearrange("p (t m j) -> p m j t", t=2, j=PACK), in_=src[:, :, :, 2:4]
+                out=grouped[1].rearrange("p (t m j) -> p m j t", t=2, j=PACK), in_=src[:, :, :, 2:4]
             )
             for u in range(2):
                 w1c[z][u] = sb("w1c%d_%d" % (z, u), [P, 2 * P], U32)
                 w1s[z][u] = sb("w1s%d_%d" % (z, u), [P, 2 * P], U8)
-                nc.vector.quantize_mx(out=w1c[z][u][:].bitcast(FP8X4), scales=w1s[z][u][:], in_=grouped[u][:])
+                nc.vector.quantize_mx(out=w1c[z][u][:].bitcast(FP8X4), scales=w1s[z][u][:], in_=grouped[u])
 
         xg = [sb("xg%d" % z, [P, S], U32) for z in range(PASSES)]
         nc.vector.tensor_copy(out=xg[0][:], in_=xw[0][:].indirect(offs_t[:]))
@@ -102,34 +110,26 @@ def tile_picked_devox_none_p_kernel(
             nc.vector.tensor_copy(out=xg[1][:, lo:hi], in_=xw[1][:].indirect(entries(offs_t, lo, hi)))
 
         emb_v = emb.rearrange("(p t) r -> p t r", t=PACK)
-        emb1 = sb("emb1", [P, U], F32, "w1g1_1")
+        emb1 = sb("emb1", [P, U], F32, "w1_raw1")
         nc.sync.dma_start(out=emb1[:], in_=emb_v[:, 1, :])
-        wide3 = sb("wide3", [P, 2 * U], F32, "xw0")
-        nc.gpsimd.memset(wide3[:, 0:U], 0.0)
         nc.sync.dma_start(out=wide3[:, U:], in_=emb_v[:, 2, :])
-        wide2 = sb("wide2", [P, 2 * U], F32, "xw1")
-        nc.gpsimd.memset(wide2[:, 0:U], 0.0)
         nc.sync.dma_start(out=wide2[:, U:], in_=emb_v[:, 3, :])
-        up = [win[0], win[1], wide2, wide3]
 
-        def first_product(acc, t, lo, hi):
+        def first_product(acc, z, t, lo, hi):
             u, e = divmod(t, 2)
             cuts = [lo, 256, hi] if lo == 128 else [lo, hi]
-            for z in range(PASSES):
-                for a, b in zip(cuts, cuts[1:]):
-                    nc.tensor.matmul_mx(
-                        out=acc[:, a - lo : b - lo],
-                        lhsT=w1c[z][u][:, e * P : (e + 1) * P].bitcast(FP8X4),
-                        lhsT_scale=w1s[z][u][:, e * P : (e + 1) * P],
-                        rhs=xg[z][:, a:b].bitcast(FP8X4),
-                        rhs_scale=xs_at[:, z * S + a : z * S + b],
-                        start=(z == 0 and a == lo),
-                        stop=(z == PASSES - 1 and b == hi),
-                    )
+            for a, b in zip(cuts, cuts[1:]):
+                nc.tensor.matmul_mx(
+                    out=acc[:, a - lo : b - lo],
+                    lhsT=w1c[z][u][:, e * P : (e + 1) * P].bitcast(FP8X4),
+                    lhsT_scale=w1s[z][u][:, e * P : (e + 1) * P],
+                    rhs=xg[z][:, a:b].bitcast(FP8X4),
+                    rhs_scale=xs_at[:, z * S + a : z * S + b],
+                    start=(z == 0 and a == lo),
+                    stop=(z == PASSES - 1 and b == hi),
+                )
 
-        def rectify(t, lo, hi, b, on_scalar):
-            acc = bank(b)
-            first_product(acc, t, lo, hi)
+        def rectify(acc, t, lo, hi, on_scalar):
             h = sb("h%d_%d" % (t, lo), [P, hi - lo], F32)[:]
             if on_scalar:
                 nc.scalar.activation(out=h, in_=acc[:, 0 : hi - lo], func=RELU)
@@ -144,24 +144,23 @@ def tile_picked_devox_none_p_kernel(
             else:
                 nc.vector.tensor_copy(out=target, in_=h)
 
-        h10 = rectify(1, 0, 128, 0, True)
-        place(1, h10, 0, 128)
-        h00 = rectify(0, 0, 256, 1, False)
-        place(0, h00, 0, 256)
-        h11 = rectify(1, 128, 512, 2, True)
-        h30 = rectify(3, 0, 256, 3, True)
+        pieces = [(1, 0, 128), (1, 128, 512), (0, 0, 256), (0, 256, 512), (2, 0, 512), (3, 0, 512)]
+        accs = [bank(b) for b in range(len(pieces))]
+        for n, z in ((0, 0), (0, 1), (1, 0), (2, 0), (1, 1), (2, 1), (3, 0), (3, 1), (4, 0), (4, 1), (5, 0), (5, 1)):
+            first_product(accs[n], z, *pieces[n])
+        place(1, rectify(accs[0], *pieces[0], True), 0, 128)
+        h11 = rectify(accs[1], *pieces[1], False)
+        h00 = rectify(accs[2], *pieces[2], True)
         place(1, h11, 128, 512)
-        h01 = rectify(0, 256, 512, 4, False)
-        h20 = rectify(2, 0, 256, 5, False)
-        place(0, h01, 256, 512)
-        h31 = rectify(3, 256, 512, 6, True)
-        place(3, h30, 0, 256)
-        place(2, h20, 0, 256)
+        place(0, h00, 0, 256)
+        place(0, rectify(accs[3], *pieces[3], False), 256, 512)
+        h2 = rectify(accs[4], *pieces[4], True)
+        h3 = rectify(accs[5], *pieces[5], True)
+        place(2, h2, 0, 512)
+        place(3, h3[:, 0:256], 0, 256)
+        place(3, h3[:, 256:512], 256, 512)
         pairs = sb("pairs", [P, 2 * U], F32, "w1c1_0")
         nc.sync.dma_start(out=pairs[:, U:], in_=emb_v[:, 0, :])
-        h21 = rectify(2, 256, 512, 7, True)
-        place(3, h31, 256, 512)
-        place(2, h21, 256, 512)
 
         embs = [pairs[:, U:], emb1[:]]
         w2w = sb("w2w", [P, N], U32, "xg0")
@@ -205,7 +204,7 @@ def tile_picked_devox_none_p_kernel(
                 in_=pairs[:].rearrange("p (u r) -> p r u", u=2)[:, lo:hi],
             )
 
-        y = sb("y", [P, U], F32, "xw1")
+        y = sb("y", [P, U], F32, "wide2")
 
         def second_product(c, acc):
             lo, hi = chunks[c]
@@ -222,7 +221,7 @@ def tile_picked_devox_none_p_kernel(
                 stop=True,
             )
 
-        accs = [bank(0), bank(1), bank(2)]
+        accs = [bank(6), bank(7), bank(0)]
         weave(0)
         weave(1)
         second_product(0, accs[0][:, 0:256])

@@ -144,21 +144,34 @@ def tile_picked_devox_none_p_kernel(
             else:
                 nc.vector.tensor_copy(out=target, in_=h)
 
-        pieces = [(1, 0, 128), (1, 128, 512), (0, 0, 256), (0, 256, 512), (2, 0, 512), (3, 0, 512)]
-        accs = [bank(b) for b in range(len(pieces))]
-        for n, z in ((0, 0), (0, 1), (1, 0), (2, 0), (1, 1), (2, 1), (3, 0), (3, 1), (4, 0), (4, 1), (5, 0), (5, 1)):
-            first_product(accs[n], z, *pieces[n])
-        place(1, rectify(accs[0], *pieces[0], True), 0, 128)
-        h11 = rectify(accs[1], *pieces[1], False)
-        h00 = rectify(accs[2], *pieces[2], True)
-        place(1, h11, 128, 512)
-        place(0, h00, 0, 256)
-        place(0, rectify(accs[3], *pieces[3], False), 256, 512)
-        h2 = rectify(accs[4], *pieces[4], True)
-        h3 = rectify(accs[5], *pieces[5], True)
+        def produce(b, t, lo, hi, on_scalar):
+            acc = bank(b)
+            for z in range(PASSES):
+                first_product(acc, z, t, lo, hi)
+            return rectify(acc, t, lo, hi, on_scalar)
+
+        firsts = [bank(0), bank(1)]
+        for z in range(PASSES):
+            for t in (1, 0):
+                first_product(firsts[t], z, t, 0, 128)
+        h10 = rectify(firsts[1], 1, 0, 128, True)
+        h00 = rectify(firsts[0], 0, 0, 128, True)
+        place(1, h10, 0, 128)
+        place(0, h00, 0, 128)
+        h11 = produce(2, 1, 128, 384, False)
+        h01 = produce(3, 0, 128, 384, True)
+        place(1, h11, 128, 384)
+        place(0, h01, 128, 384)
+        h12 = produce(4, 1, 384, 512, False)
+        h02 = produce(5, 0, 384, 512, True)
+        h30 = produce(6, 3, 0, 256, False)
+        place(1, h12, 384, 512)
+        place(0, h02, 384, 512)
+        h2 = produce(7, 2, 0, 512, True)
+        h31 = produce(0, 3, 256, 512, False)
+        place(3, h30, 0, 256)
         place(2, h2, 0, 512)
-        place(3, h3[:, 0:256], 0, 256)
-        place(3, h3[:, 256:512], 256, 512)
+        place(3, h31, 256, 512)
         pairs = sb("pairs", [P, 2 * U], F32, "w1c1_0")
         nc.sync.dma_start(out=pairs[:, U:], in_=emb_v[:, 0, :])
 
@@ -221,7 +234,7 @@ def tile_picked_devox_none_p_kernel(
                 stop=True,
             )
 
-        accs = [bank(6), bank(7), bank(0)]
+        accs = [bank(1), bank(2), bank(3)]
         weave(0)
         weave(1)
         second_product(0, accs[0][:, 0:256])
@@ -236,7 +249,7 @@ def tile_picked_devox_none_p_kernel(
         nc.vector.tensor_copy(out=y[:, 512:896], in_=accs[1][:, 0:384])
         nc.scalar.copy(out=y[:, 896:1024], in_=accs[2][:, 0:128])
 
-        parts = [(0, 384), (384, 512)]
+        parts = [(0, 256), (256, 512)]
         first = [sb("first%d" % a, [P, hi - lo], F32) for a, (lo, hi) in enumerate(parts)]
         second = [sb("second%d" % a, [P, hi - lo], F32) for a, (lo, hi) in enumerate(parts)]
         for a, (lo, hi) in enumerate(parts):

@@ -20,7 +20,6 @@ COPY = mybir.ActivationFunctionType.Copy
 P = 128
 PACK = 4
 PASSES = 2
-LINE = 4
 
 
 def tile_picked_devox_none_p_kernel(
@@ -196,10 +195,9 @@ def tile_picked_devox_none_p_kernel(
             engine.tensor_tensor(out=half, in0=up[t][:, lo:hi], in1=embs[t][:, lo:hi], op=ADD)
 
         def add_high(lo, hi):
-            lines = slice(lo // LINE, hi // LINE)
-            a = wide2[:].rearrange("p (e c i) -> p c e i", e=2, i=LINE)[:, lines]
-            b = wide3[:].rearrange("p (e c i) -> p c e i", e=2, i=LINE)[:, lines, ::-1, :]
-            both = words(1, lo, hi).bitcast(BF16).rearrange("p (c i e) -> p c e i", e=2, i=LINE)
+            a = wide2[:].rearrange("p (e r) -> p r e", e=2)[:, lo:hi]
+            b = wide3[:].rearrange("p (e r) -> p r e", e=2)[:, lo:hi, ::-1]
+            both = words(1, lo, hi).bitcast(BF16).rearrange("p (r e) -> p r e", e=2)
             nc.vector.tensor_tensor(out=both, in0=a, in1=b, op=ADD)
 
         for t in (1, 0):

@@ -105,7 +105,7 @@ def tile_picked_devox_none_p_kernel(
 
         xg = [sb("xg%d" % z, [P, S], U32) for z in range(PASSES)]
         nc.vector.tensor_copy(out=xg[0][:], in_=xw[0][:].indirect(offs_t[:]))
-        for lo, hi in ((0, 128), (128, 256), (256, 512)):
+        for lo, hi in ((0, 128), (128, 384), (384, 512)):
             nc.vector.tensor_copy(out=xg[1][:, lo:hi], in_=xw[1][:].indirect(entries(offs_t, lo, hi)))
 
         emb_v = emb.rearrange("(p t) r -> p t r", t=PACK)
@@ -116,17 +116,15 @@ def tile_picked_devox_none_p_kernel(
 
         def first_product(acc, z, t, lo, hi):
             u, e = divmod(t, 2)
-            cuts = [lo, 256, hi] if lo == 128 else [lo, hi]
-            for a, b in zip(cuts, cuts[1:]):
-                nc.tensor.matmul_mx(
-                    out=acc[:, a - lo : b - lo],
-                    lhsT=w1c[z][u][:, e * P : (e + 1) * P].bitcast(FP8X4),
-                    lhsT_scale=w1s[z][u][:, e * P : (e + 1) * P],
-                    rhs=xg[z][:, a:b].bitcast(FP8X4),
-                    rhs_scale=xs_at[:, z * S + a : z * S + b],
-                    start=(z == 0 and a == lo),
-                    stop=(z == PASSES - 1 and b == hi),
-                )
+            nc.tensor.matmul_mx(
+                out=acc[:, 0 : hi - lo],
+                lhsT=w1c[z][u][:, e * P : (e + 1) * P].bitcast(FP8X4),
+                lhsT_scale=w1s[z][u][:, e * P : (e + 1) * P],
+                rhs=xg[z][:, lo:hi].bitcast(FP8X4),
+                rhs_scale=xs_at[:, z * S + lo : z * S + hi],
+                start=(z == 0),
+                stop=(z == PASSES - 1),
+            )
 
         def rectify(acc, t, lo, hi, on_scalar):
             h = sb("h%d_%d" % (t, lo), [P, hi - lo], F32)[:]
@@ -203,7 +201,7 @@ def tile_picked_devox_none_p_kernel(
         for t in (1, 0):
             add_low(nc.gpsimd, t, 0, U)
 
-        edges = (0, 256, 512, 768, 896, 1024)
+        edges = (0, 256, 512, 768, 896, 960, 1024)
         chunks = list(zip(edges, edges[1:]))
         zq = [sb("zi%d" % c, [P, (hi - lo) * PACK], BF16) for c, (lo, hi) in enumerate(chunks)]
 
@@ -240,10 +238,12 @@ def tile_picked_devox_none_p_kernel(
         second_product(1, accs[0][:, 256:512])
         weave(3)
         weave(4)
+        weave(5)
         second_product(2, accs[1][:, 0:256])
         nc.scalar.copy(out=y[:, 0:512], in_=accs[0][:])
         second_product(3, accs[1][:, 256:384])
-        second_product(4, accs[2][:, 0:128])
+        second_product(4, accs[2][:, 0:64])
+        second_product(5, accs[2][:, 64:128])
         nc.vector.tensor_copy(out=y[:, 512:896], in_=accs[1][:, 0:384])
         nc.scalar.copy(out=y[:, 896:1024], in_=accs[2][:, 0:128])
 

@@ -20,6 +20,7 @@ COPY = mybir.ActivationFunctionType.Copy
 P = 128
 PACK = 4
 PASSES = 2
+SHARE = 192
 
 
 def tile_picked_devox_none_p_kernel(
@@ -91,7 +92,7 @@ def tile_picked_devox_none_p_kernel(
             if z == 0:
                 grouped = [sb("w1g%d" % u, [P, 2 * P * PACK], BF16)[:] for u in range(2)]
             else:
-                grouped = [wide[:, U : U + P * PACK].bitcast(BF16) for wide in (wide3, wide2)]
+                grouped = [wide[:, U : U + P * PACK].bitcast(BF16) for wide in (wide2, wide3)]
             nc.scalar.copy(
                 out=grouped[0].rearrange("p (t m j) -> p m j t", t=2, j=PACK), in_=src[:, :, :, 0:2]
             )
@@ -111,8 +112,8 @@ def tile_picked_devox_none_p_kernel(
         emb_v = emb.rearrange("(p t) r -> p t r", t=PACK)
         emb1 = sb("emb1", [P, U], F32, "w1_raw1")
         nc.sync.dma_start(out=emb1[:], in_=emb_v[:, 1, :])
-        nc.sync.dma_start(out=wide3[:, U:], in_=emb_v[:, 2, :])
         nc.sync.dma_start(out=wide2[:, U:], in_=emb_v[:, 3, :])
+        nc.sync.dma_start(out=wide3[:, U:], in_=emb_v[:, 2, :])
 
         def first_product(acc, z, t, lo, hi):
             u, e = divmod(t, 2)
@@ -126,8 +127,9 @@ def tile_picked_devox_none_p_kernel(
                 stop=(z == PASSES - 1),
             )
 
-        def rectify(acc, t, lo, hi, on_scalar):
-            h = sb("h%d_%d" % (t, lo), [P, hi - lo], F32)[:]
+        def rectify(acc, t, lo, hi, on_scalar, h=None):
+            if h is None:
+                h = sb("h%d_%d" % (t, lo), [P, hi - lo], F32)[:]
             if on_scalar:
                 nc.scalar.activation(out=h, in_=acc[:, 0 : hi - lo], func=RELU)
             else:
@@ -141,11 +143,11 @@ def tile_picked_devox_none_p_kernel(
             else:
                 nc.vector.tensor_copy(out=target, in_=h)
 
-        def produce(b, t, lo, hi, on_scalar):
+        def produce(b, t, lo, hi, on_scalar, h=None):
             acc = bank(b)
             for z in range(PASSES):
                 first_product(acc, z, t, lo, hi)
-            return rectify(acc, t, lo, hi, on_scalar)
+            return rectify(acc, t, lo, hi, on_scalar, h)
 
         firsts = [bank(0), bank(1)]
         for z in range(PASSES):
@@ -161,7 +163,9 @@ def tile_picked_devox_none_p_kernel(
         place(0, h01, 128, 384)
         h12 = produce(4, 1, 384, 512, False)
         h02 = produce(5, 0, 384, 512, True)
-        h30 = produce(6, 3, 0, 256, False)
+        pairs = sb("pairs", [P, 2 * U + SHARE], F32, "w1c1_0")
+        nc.sync.dma_start(out=pairs[:, U + SHARE :], in_=emb_v[:, 0, :])
+        h30 = produce(6, 3, 0, 256, False, pairs[:, U - SHARE : U - SHARE + 256])
         place(1, h12, 384, 512)
         place(0, h02, 384, 512)
         h2 = produce(7, 2, 0, 512, True)
@@ -169,10 +173,8 @@ def tile_picked_devox_none_p_kernel(
         place(3, h30, 0, 256)
         place(2, h2, 0, 512)
         place(3, h31, 256, 512)
-        pairs = sb("pairs", [P, 2 * U], F32, "w1c1_0")
-        nc.sync.dma_start(out=pairs[:, U:], in_=emb_v[:, 0, :])
 
-        embs = [pairs[:, U:], emb1[:]]
+        embs = [pairs[:, U + SHARE :], emb1[:]]
         w2w = sb("w2w", [P, N], U32, "xg0")
         nc.sync.dma_start(out=w2w[:].bitcast(I32), in_=w2_words[0].rearrange("p n t -> p (n t)").bitcast(I32))
         w2s = sb("w2s", [P, N], U8, "w1s0_0")
@@ -199,7 +201,9 @@ def tile_picked_devox_none_p_kernel(
             nc.vector.tensor_tensor(out=both, in0=a, in1=b, op=ADD)
 
         for t in (1, 0):
-            add_low(nc.gpsimd, t, 0, U)
+            add_low(nc.gpsimd, t, 0, U - SHARE)
+        for t in (1, 0):
+            add_low(nc.vector, t, U - SHARE, U)
 
         edges = (0, 256, 512, 768, 896, 960, 1024)
         chunks = list(zip(edges, edges[1:]))
@@ -210,7 +214,7 @@ def tile_picked_devox_none_p_kernel(
             add_high(lo, hi)
             nc.scalar.copy(
                 out=zq[c][:].bitcast(F32).rearrange("p (r u) -> p r u", u=2),
-                in_=pairs[:].rearrange("p (u r) -> p r u", u=2)[:, lo:hi],
+                in_=pairs[:, 0 : 2 * U].rearrange("p (u r) -> p r u", u=2)[:, lo:hi],
             )
 
         y = sb("y", [P, U], F32, "wide2")

@@ -213,8 +213,8 @@ def tile_picked_devox_none_p_kernel(
             lo, hi = chunks[c]
             add_high(lo, hi)
             nc.scalar.copy(
-                out=zq[c][:].bitcast(F32).rearrange("p (r u) -> p r u", u=2),
-                in_=pairs[:, 0 : 2 * U].rearrange("p (u r) -> p r u", u=2)[:, lo:hi],
+                out=zq[c][:].bitcast(F32).rearrange("p (r i u) -> p r u i", u=2, i=2),
+                in_=pairs[:, 0 : 2 * U].rearrange("p (u r i) -> p r u i", u=2, i=2)[:, lo // 2 : hi // 2],
             )
 
         y = sb("y", [P, U], F32, "wide2")

@@ -20,7 +20,7 @@ COPY = mybir.ActivationFunctionType.Copy
 P = 128
 PACK = 4
 PASSES = 2
-SHARE = 192
+SHARE = 320
 
 
 def tile_picked_devox_none_p_kernel(

@@ -1,6 +1,7 @@
 from contextlib import ExitStack
 
 import concourse.mybir as mybir
+from concourse.masks import make_identity
 
 K, T, S, V, H, N, U = 1024, 2048, 512, 512, 512, 128, 1024
 FLOPS = 2 * K * H * S + 2 * H * N * U
@@ -20,7 +21,7 @@ COPY = mybir.ActivationFunctionType.Copy
 P = 128
 PACK = 4
 PASSES = 2
-SHARE = 320
+TURNED = 128
 
 
 def tile_picked_devox_none_p_kernel(
@@ -110,10 +111,13 @@ def tile_picked_devox_none_p_kernel(
             nc.vector.tensor_copy(out=xg[1][:, lo:hi], in_=xw[1][:].indirect(entries(offs_t, lo, hi)))
 
         emb_v = emb.rearrange("(p t) r -> p t r", t=PACK)
-        emb1 = sb("emb1", [P, U], F32, "w1_raw1")
-        nc.sync.dma_start(out=emb1[:], in_=emb_v[:, 1, :])
-        nc.sync.dma_start(out=wide2[:, U:], in_=emb_v[:, 3, :])
-        nc.sync.dma_start(out=wide3[:, U:], in_=emb_v[:, 2, :])
+        plain = U - TURNED
+        tails = sb("tails", [P, PACK, TURNED], F32, "w1_raw1")
+        nc.sync.dma_start(out=tails[:], in_=emb_v[:, :, plain:U])
+        nc.sync.dma_start(out=wide2[:, U : U + plain], in_=emb_v[:, 3, 0:plain])
+        nc.sync.dma_start(out=wide3[:, U : U + plain], in_=emb_v[:, 2, 0:plain])
+        emb_low = sb("emb_low", [P, 2, plain], F32, "xw0")
+        nc.sync.dma_start(out=emb_low[:], in_=emb_v[:, 0:2, 0:plain])
 
         def first_product(acc, z, t, lo, hi):
             u, e = divmod(t, 2)
@@ -163,18 +167,33 @@ def tile_picked_devox_none_p_kernel(
         place(0, h01, 128, 384)
         h12 = produce(4, 1, 384, 512, False)
         h02 = produce(5, 0, 384, 512, True)
-        pairs = sb("pairs", [P, 2 * U + SHARE], F32, "w1c1_0")
-        nc.sync.dma_start(out=pairs[:, U + SHARE :], in_=emb_v[:, 0, :])
-        h30 = produce(6, 3, 0, 256, False, pairs[:, U - SHARE : U - SHARE + 256])
+        h30 = produce(6, 3, 0, 256, False)
         place(1, h12, 384, 512)
         place(0, h02, 384, 512)
         h2 = produce(7, 2, 0, 512, True)
         h31 = produce(0, 3, 256, 512, False)
+        ident = sb("ident", [P, P], F32, "xw1")
+        make_identity(nc, ident[:])
+        sums = [bank(4), bank(5)]
+
+        def turn(t, source, opens=False, closes=False):
+            nc.tensor.matmul(
+                out=sums[t // 2][:, t % 2 * P : (t % 2 + 1) * P],
+                lhsT=source,
+                rhs=ident[:],
+                is_transpose=True,
+                start=opens,
+                stop=closes,
+            )
+
+        for t in range(PACK):
+            turn(t, tails[:, t, :], opens=(t % 2 == 0))
         place(3, h30, 0, 256)
         place(2, h2, 0, 512)
         place(3, h31, 256, 512)
 
-        embs = [pairs[:, U + SHARE :], emb1[:]]
+        embs = [emb_low[:, 0, :], emb_low[:, 1, :]]
+        pairs = sb("pairs", [P, 2 * plain], F32)
         w2w = sb("w2w", [P, N], U32, "xg0")
         nc.sync.dma_start(out=w2w[:].bitcast(I32), in_=w2_words[0].rearrange("p n t -> p (n t)").bitcast(I32))
         w2s = sb("w2s", [P, N], U8, "w1s0_0")
@@ -188,7 +207,7 @@ def tile_picked_devox_none_p_kernel(
         nc.sync.dma_start(out=gate_t[:], in_=gate.rearrange("d p v -> p d v"))
 
         def words(u, lo, hi):
-            return pairs[:, u * U + lo : u * U + hi]
+            return pairs[:, u * plain + lo : u * plain + hi]
 
         def add_low(engine, t, lo, hi):
             half = words(0, lo, hi).bitcast(BF16).rearrange("p (r e) -> p r e", e=2)[:, :, t]
@@ -201,27 +220,42 @@ def tile_picked_devox_none_p_kernel(
             nc.vector.tensor_tensor(out=both, in0=a, in1=b, op=ADD)
 
         for t in (1, 0):
-            add_low(nc.gpsimd, t, 0, U - SHARE)
-        for t in (1, 0):
-            add_low(nc.vector, t, U - SHARE, U)
+            add_low(nc.gpsimd, t, 0, plain)
 
-        edges = (0, 256, 512, 768, 896, 960, 1024)
-        chunks = list(zip(edges, edges[1:]))
-        zq = [sb("zi%d" % c, [P, (hi - lo) * PACK], BF16) for c, (lo, hi) in enumerate(chunks)]
+        turn(1, up[1][:, plain:U])
+        turn(0, up[0][:, plain:U], closes=True)
+        turned = sb("turned", [P, 2 * P], F32, "h3_256")
 
-        def weave(c):
-            lo, hi = chunks[c]
-            add_high(lo, hi)
+        def round_half(u):
             nc.scalar.copy(
+                out=turned[:, u * P : (u + 1) * P].bitcast(BF16).rearrange("c (p e) -> c p e", e=2),
+                in_=sums[u][:, 0 : 2 * P].rearrange("c (e p) -> c p e", e=2),
+            )
+
+        round_half(0)
+        turn(2, up[2][:, plain:U])
+        turn(3, up[3][:, plain:U], closes=True)
+        round_half(1)
+        back = bank(5)
+        for u in range(2):
+            nc.tensor.transpose(back[:, u * P : (u + 1) * P], turned[:, u * P : (u + 1) * P], ident[:])
+
+        edges = (0, 256, 512, 768, 896, 1024)
+        chunks = list(zip(edges, edges[1:]))
+        zq = [sb("zi%d" % c, [P, (hi - lo) * PACK], BF16) for c, (lo, hi) in enumerate(chunks[:-1])]
+
+        def weave(c, copy):
+            lo, hi = chunks[c]
+            copy(
                 out=zq[c][:].bitcast(F32).rearrange("p (r i u) -> p r u i", u=2, i=2),
-                in_=pairs[:, 0 : 2 * U].rearrange("p (u r i) -> p r u i", u=2, i=2)[:, lo // 2 : hi // 2],
+                in_=pairs[:].rearrange("p (u r i) -> p r u i", u=2, i=2)[:, lo // 2 : hi // 2],
             )
 
         y = sb("y", [P, U], F32, "wide2")
 
         def second_product(c, acc):
             lo, hi = chunks[c]
-            zc = sb("zc%d" % c, [P, hi - lo], U32)
+            zc = sb("zc%d" % c, [P, hi - lo], U32, "pairs" if c == 3 else None)
             zs = sb("zs%d" % c, [P, hi - lo], U8)
             nc.vector.quantize_mx(out=zc[:].bitcast(FP8X4), scales=zs[:], in_=zq[c][:])
             nc.tensor.matmul_mx(
@@ -234,22 +268,22 @@ def tile_picked_devox_none_p_kernel(
                 stop=True,
             )
 
-        accs = [bank(1), bank(2), bank(3)]
-        weave(0)
-        weave(1)
+        accs = [bank(b) for b in (1, 2, 3, 7, 0)]
+        for c in (0, 1, 3, 2):
+            add_high(*chunks[c])
+        for c in (0, 1, 2):
+            weave(c, nc.scalar.copy)
+        weave(3, nc.vector.tensor_copy)
         second_product(0, accs[0][:, 0:256])
-        weave(2)
-        second_product(1, accs[0][:, 256:512])
-        weave(3)
-        weave(4)
-        weave(5)
-        second_product(2, accs[1][:, 0:256])
-        nc.scalar.copy(out=y[:, 0:512], in_=accs[0][:])
-        second_product(3, accs[1][:, 256:384])
-        second_product(4, accs[2][:, 0:64])
-        second_product(5, accs[2][:, 64:128])
-        nc.vector.tensor_copy(out=y[:, 512:896], in_=accs[1][:, 0:384])
-        nc.scalar.copy(out=y[:, 896:1024], in_=accs[2][:, 0:128])
+        zq.append(sb("zi4", [P, TURNED * PACK], BF16, "xw0"))
+        nc.scalar.copy(
+            out=zq[4][:].bitcast(F32).rearrange("p (r u) -> p r u", u=2),
+            in_=back[:, 0 : 2 * P].rearrange("p (u r) -> p r u", u=2),
+        )
+        for c in range(1, len(chunks)):
+            second_product(c, accs[c][:, 0 : chunks[c][1] - chunks[c][0]])
+        for c, (lo, hi) in enumerate(chunks):
+            (nc.vector.tensor_copy if c == 3 else nc.scalar.copy)(out=y[:, lo:hi], in_=accs[c][:, 0 : hi - lo])
 
         parts = [(0, 256), (256, 512)]
         first = [sb("first%d" % a, [P, hi - lo], F32) for a, (lo, hi) in enumerate(parts)]

@@ -22,6 +22,7 @@ P = 128
 PACK = 4
 PASSES = 2
 TURNED = 128
+SHARE = 64
 
 
 def tile_picked_devox_none_p_kernel(
@@ -112,12 +113,12 @@ def tile_picked_devox_none_p_kernel(
 
         emb_v = emb.rearrange("(p t) r -> p t r", t=PACK)
         plain = U - TURNED
-        tails = sb("tails", [P, PACK, TURNED], F32, "w1_raw1")
+        tails = sb("tails", [P, PACK, TURNED], F32, "w1_raw0")
         nc.sync.dma_start(out=tails[:], in_=emb_v[:, :, plain:U])
+        emb_low = sb("emb_low", [P, 2, plain], F32, "w1_raw1")
+        nc.sync.dma_start(out=emb_low[:], in_=emb_v[:, 0:2, 0:plain])
         nc.sync.dma_start(out=wide2[:, U : U + plain], in_=emb_v[:, 3, 0:plain])
         nc.sync.dma_start(out=wide3[:, U : U + plain], in_=emb_v[:, 2, 0:plain])
-        emb_low = sb("emb_low", [P, 2, plain], F32, "xw0")
-        nc.sync.dma_start(out=emb_low[:], in_=emb_v[:, 0:2, 0:plain])
 
         def first_product(acc, z, t, lo, hi):
             u, e = divmod(t, 2)
@@ -167,7 +168,8 @@ def tile_picked_devox_none_p_kernel(
         place(0, h01, 128, 384)
         h12 = produce(4, 1, 384, 512, False)
         h02 = produce(5, 0, 384, 512, True)
-        h30 = produce(6, 3, 0, 256, False)
+        pairs = sb("pairs", [P, 2 * plain], F32)
+        h30 = produce(6, 3, 0, 256, False, pairs[:, plain - SHARE : plain - SHARE + 256])
         place(1, h12, 384, 512)
         place(0, h02, 384, 512)
         h2 = produce(7, 2, 0, 512, True)
@@ -193,7 +195,6 @@ def tile_picked_devox_none_p_kernel(
         place(3, h31, 256, 512)
 
         embs = [emb_low[:, 0, :], emb_low[:, 1, :]]
-        pairs = sb("pairs", [P, 2 * plain], F32)
         w2w = sb("w2w", [P, N], U32, "xg0")
         nc.sync.dma_start(out=w2w[:].bitcast(I32), in_=w2_words[0].rearrange("p n t -> p (n t)").bitcast(I32))
         w2s = sb("w2s", [P, N], U8, "w1s0_0")
@@ -220,7 +221,9 @@ def tile_picked_devox_none_p_kernel(
             nc.vector.tensor_tensor(out=both, in0=a, in1=b, op=ADD)
 
         for t in (1, 0):
-            add_low(nc.gpsimd, t, 0, plain)
+            add_low(nc.gpsimd, t, 0, plain - SHARE)
+        for t in (1, 0):
+            add_low(nc.vector, t, plain - SHARE, plain)
 
         turn(1, up[1][:, plain:U])
         turn(0, up[0][:, plain:U], closes=True)
@@ -275,7 +278,7 @@ def tile_picked_devox_none_p_kernel(
             weave(c, nc.scalar.copy)
         weave(3, nc.vector.tensor_copy)
         second_product(0, accs[0][:, 0:256])
-        zq.append(sb("zi4", [P, TURNED * PACK], BF16, "xw0"))
+        zq.append(sb("zi4", [P, TURNED * PACK], BF16, "w1_raw1"))
         nc.scalar.copy(
             out=zq[4][:].bitcast(F32).rearrange("p (r u) -> p r u", u=2),
             in_=back[:, 0 : 2 * P].rearrange("p (u r) -> p r u", u=2),

@@ -76,6 +76,9 @@ def tile_picked_devox_none_p_kernel(
             nc.vector.memset(win[t][:], 0.0)
         for wide in (wide3, wide2):
             nc.scalar.copy(out=wide[:, 0:U], in_=win[0][:])
+        ident = sb("ident", [P, P], F32)
+        nc.vector.memset(ident[:], 0.0)
+        make_identity(nc, ident[:], nomemset=True)
 
         xs_g = sb("xs_g", [P, PASSES * S], U8)
         for z in range(PASSES):
@@ -174,8 +177,6 @@ def tile_picked_devox_none_p_kernel(
         place(0, h02, 384, 512)
         h2 = produce(7, 2, 0, 512, True)
         h31 = produce(0, 3, 256, 512, False)
-        ident = sb("ident", [P, P], F32, "xw1")
-        make_identity(nc, ident[:])
         sums = [bank(4), bank(5)]
 
         def turn(t, source, opens=False, closes=False):

@@ -177,7 +177,7 @@ def tile_picked_devox_none_p_kernel(
         place(0, h02, 384, 512)
         h2 = produce(7, 2, 0, 512, True)
         h31 = produce(0, 3, 256, 512, False)
-        sums = [bank(4), bank(5)]
+        sums = [bank(6), bank(7)]
 
         def turn(t, source, opens=False, closes=False):
             nc.tensor.matmul(
@@ -240,18 +240,18 @@ def tile_picked_devox_none_p_kernel(
         turn(2, up[2][:, plain:U])
         turn(3, up[3][:, plain:U], closes=True)
         round_half(1)
-        back = bank(5)
+        back = bank(7)
         for u in range(2):
             nc.tensor.transpose(back[:, u * P : (u + 1) * P], turned[:, u * P : (u + 1) * P], ident[:])
 
         edges = (0, 256, 512, 768, 896, 1024)
         chunks = list(zip(edges, edges[1:]))
-        zq = [sb("zi%d" % c, [P, (hi - lo) * PACK], BF16) for c, (lo, hi) in enumerate(chunks[:-1])]
+        zq = [sb("zi%d" % c, [P, (hi - lo) * PACK], BF16)[:] for c, (lo, hi) in enumerate(chunks[:3])]
 
         def weave(c, copy):
             lo, hi = chunks[c]
             copy(
-                out=zq[c][:].bitcast(F32).rearrange("p (r i u) -> p r u i", u=2, i=2),
+                out=zq[c].bitcast(F32).rearrange("p (r i u) -> p r u i", u=2, i=2),
                 in_=pairs[:].rearrange("p (u r i) -> p r u i", u=2, i=2)[:, lo // 2 : hi // 2],
             )
 
@@ -261,7 +261,7 @@ def tile_picked_devox_none_p_kernel(
             lo, hi = chunks[c]
             zc = sb("zc%d" % c, [P, hi - lo], U32, "pairs" if c == 3 else None)
             zs = sb("zs%d" % c, [P, hi - lo], U8)
-            nc.vector.quantize_mx(out=zc[:].bitcast(FP8X4), scales=zs[:], in_=zq[c][:])
+            nc.vector.quantize_mx(out=zc[:].bitcast(FP8X4), scales=zs[:], in_=zq[c])
             nc.tensor.matmul_mx(
                 out=acc,
                 lhsT=w2w[:].bitcast(FP8X4),
@@ -272,16 +272,17 @@ def tile_picked_devox_none_p_kernel(
                 stop=True,
             )
 
-        accs = [bank(b) for b in (1, 2, 3, 7, 0)]
+        accs = [bank(b) for b in (1, 2, 3, 4, 5)]
         for c in (0, 1, 3, 2):
             add_high(*chunks[c])
         for c in (0, 1, 2):
             weave(c, nc.scalar.copy)
-        weave(3, nc.vector.tensor_copy)
         second_product(0, accs[0][:, 0:256])
-        zq.append(sb("zi4", [P, TURNED * PACK], BF16, "w1_raw1"))
+        last = sb("last", [P, 2 * TURNED * PACK], BF16, "wide3")
+        zq.extend([last[:, 0 : TURNED * PACK], last[:, TURNED * PACK :]])
+        weave(3, nc.vector.tensor_copy)
         nc.scalar.copy(
-            out=zq[4][:].bitcast(F32).rearrange("p (r u) -> p r u", u=2),
+            out=zq[4].bitcast(F32).rearrange("p (r u) -> p r u", u=2),
             in_=back[:, 0 : 2 * P].rearrange("p (u r) -> p r u", u=2),
         )
         for c in range(1, len(chunks)):

@@ -230,19 +230,15 @@ def tile_picked_devox_none_p_kernel(
         turn(0, up[0][:, plain:U], closes=True)
         turned = sb("turned", [P, 2 * P], F32, "h3_256")
 
-        def round_half(u):
-            nc.scalar.copy(
+        def round_half(u, copy):
+            copy(
                 out=turned[:, u * P : (u + 1) * P].bitcast(BF16).rearrange("c (p e) -> c p e", e=2),
                 in_=sums[u][:, 0 : 2 * P].rearrange("c (e p) -> c p e", e=2),
             )
 
-        round_half(0)
+        round_half(0, nc.scalar.copy)
         turn(2, up[2][:, plain:U])
         turn(3, up[3][:, plain:U], closes=True)
-        round_half(1)
-        back = bank(7)
-        for u in range(2):
-            nc.tensor.transpose(back[:, u * P : (u + 1) * P], turned[:, u * P : (u + 1) * P], ident[:])
 
         edges = (0, 256, 512, 768, 896, 1024)
         chunks = list(zip(edges, edges[1:]))
@@ -273,14 +269,19 @@ def tile_picked_devox_none_p_kernel(
             )
 
         accs = [bank(b) for b in (1, 2, 3, 4, 5)]
-        for c in (0, 1, 3, 2):
+        for c in (0, 1, 2):
             add_high(*chunks[c])
+        round_half(1, nc.vector.tensor_copy)
+        add_high(*chunks[3])
+        back = bank(7)
+        for u in range(2):
+            nc.tensor.transpose(back[:, u * P : (u + 1) * P], turned[:, u * P : (u + 1) * P], ident[:])
         for c in (0, 1, 2):
             weave(c, nc.scalar.copy)
         second_product(0, accs[0][:, 0:256])
         last = sb("last", [P, 2 * TURNED * PACK], BF16, "wide3")
         zq.extend([last[:, 0 : TURNED * PACK], last[:, TURNED * PACK :]])
-        weave(3, nc.vector.tensor_copy)
+        weave(3, nc.scalar.copy)
         nc.scalar.copy(
             out=zq[4].bitcast(F32).rearrange("p (r u) -> p r u", u=2),
             in_=back[:, 0 : 2 * P].rearrange("p (u r) -> p r u", u=2),

@@ -239,6 +239,10 @@ def tile_picked_devox_none_p_kernel(
         round_half(0, nc.scalar.copy)
         turn(2, up[2][:, plain:U])
         turn(3, up[3][:, plain:U], closes=True)
+        round_half(1, nc.scalar.copy)
+        back = bank(7)
+        for u in range(2):
+            nc.tensor.transpose(back[:, u * P : (u + 1) * P], turned[:, u * P : (u + 1) * P], ident[:])
 
         edges = (0, 256, 512, 768, 896, 1024)
         chunks = list(zip(edges, edges[1:]))
@@ -271,18 +275,14 @@ def tile_picked_devox_none_p_kernel(
         accs = [bank(b) for b in (1, 2, 3, 4, 5)]
         for c in (0, 1, 2):
             add_high(*chunks[c])
-        round_half(1, nc.vector.tensor_copy)
         add_high(*chunks[3])
-        back = bank(7)
-        for u in range(2):
-            nc.tensor.transpose(back[:, u * P : (u + 1) * P], turned[:, u * P : (u + 1) * P], ident[:])
         for c in (0, 1, 2):
             weave(c, nc.scalar.copy)
         second_product(0, accs[0][:, 0:256])
         last = sb("last", [P, 2 * TURNED * PACK], BF16, "wide3")
         zq.extend([last[:, 0 : TURNED * PACK], last[:, TURNED * PACK :]])
         weave(3, nc.scalar.copy)
-        nc.scalar.copy(
+        nc.vector.tensor_copy(
             out=zq[4].bitcast(F32).rearrange("p (r u) -> p r u", u=2),
             in_=back[:, 0 : 2 * P].rearrange("p (u r) -> p r u", u=2),
         )

from contextlib import ExitStack

import concourse.mybir as mybir
from concourse.masks import make_identity

K, T, S, V, H, N, U = 1024, 2048, 512, 512, 512, 128, 1024
FLOPS = 2 * K * H * S + 2 * H * N * U

F32 = mybir.dt.float32
BF16 = mybir.dt.bfloat16
I32 = mybir.dt.int32
U32 = mybir.dt.uint32
U16 = mybir.dt.uint16
U8 = mybir.dt.uint8
FP8X4 = mybir.dt.float8_e4m3fn_x4
ADD = mybir.AluOpType.add
MULT = mybir.AluOpType.mult
RELU = mybir.ActivationFunctionType.Relu
COPY = mybir.ActivationFunctionType.Copy

P = 128
PACK = 4
PASSES = 2
TURNED = 128
SHARE = 64


def tile_picked_devox_none_p_kernel(
    tc, x_words, x_scales, w1, w2_words, w2_scales, gate, emb, offs, cell, pos1, pos2, out
):
    nc = tc.nc
    with ExitStack() as ctx:
        keep = ctx.enter_context(tc.tile_pool(name="keep", bufs=1))
        psum = ctx.enter_context(tc.psum_pool(name="psum", bufs=1))

        def sb(name, shape, dtype, tag=None):
            return keep.tile(shape, dtype, name=name, tag=tag or name, align_bytes=64)

        def bank(b):
            return psum.tile([P, 512], F32, name="bank%d" % b, tag="bank%d" % b)

        def entries(lst, lo, hi):
            return lst[:, lo // 16 : hi // 16]

        offs_t = sb("offs_t", [P, S // 16], U16)
        cell_t = sb("cell_t", [P, S // 16], U16)
        pos_t = [sb("pos_t%d" % d, [P, V // 16], U16) for d in range(2)]
        xs = sb("xs", [P, PASSES * T], U8)
        w1_raw = [sb("w1_raw%d" % z, [P, PACK, H], F32) for z in range(PASSES)]
        xw = [sb("xw%d" % z, [P, T], U32) for z in range(PASSES)]
        win = [sb("win%d" % t, [P, U], F32) for t in range(2)]
        wide2 = sb("wide2", [P, 2 * U], F32)
        wide3 = sb("wide3", [P, 2 * U], F32)

        nc.vector.memset(xs[:].bitcast(I32), 0)
        for z in range(PASSES):
            nc.sync.dma_start(
                out=w1_raw[z][:], in_=w1[512 * z : 512 * (z + 1), :].rearrange("(p j) c -> p j c", j=PACK)
            )
            if z == 0:
                nc.sync.dma_start(
                    out=xs[0:P:8, :].bitcast(I32).rearrange("q (z n) -> q z n", z=PASSES),
                    in_=x_scales.rearrange("z q n -> q z n").bitcast(I32),
                )
                nc.sync.dma_start(offs_t[:], offs)
        for z in range(PASSES):
            nc.sync.dma_start(
                out=xw[z][:].bitcast(I32), in_=x_words[z].rearrange("p n t -> p (n t)").bitcast(I32)
            )
        nc.sync.dma_start(cell_t[:], cell)
        nc.sync.dma_start(pos_t[0][:], pos1)
        nc.sync.dma_start(pos_t[1][:], pos2)

        up = [win[0], win[1], wide2, wide3]
        for t in range(2):
            nc.vector.memset(win[t][:], 0.0)
        for wide in (wide3, wide2):
            nc.scalar.copy(out=wide[:, 0:U], in_=win[0][:])
        ident = sb("ident", [P, P], F32)
        nc.vector.memset(ident[:], 0.0)
        make_identity(nc, ident[:], nomemset=True)

        xs_g = sb("xs_g", [P, PASSES * S], U8)
        for z in range(PASSES):
            nc.vector.tensor_copy(
                out=xs_g[:, z * S : (z + 1) * S], in_=xs[:, z * T : (z + 1) * T].indirect(offs_t[:])
            )
        xs_at = sb("xs_at", [P, PASSES * S], U8)
        nc.vector.tensor_copy(out=xs_at[:].bitcast(I32), in_=xs_g[:].bitcast(I32))
        for r in range(1, 4):
            nc.sync.dma_start(out=xs_at[r:P:32, :].bitcast(I32), in_=xs_g[8 * r : P : 32, :].bitcast(I32))

        w1c = [[None, None] for z in range(PASSES)]
        w1s = [[None, None] for z in range(PASSES)]
        for z in range(PASSES):
            src = w1_raw[z][:].rearrange("p j (m t) -> p m j t", t=PACK)
            if z == 0:
                grouped = [sb("w1g%d" % u, [P, 2 * P * PACK], BF16)[:] for u in range(2)]
            else:
                grouped = [wide[:, U : U + P * PACK].bitcast(BF16) for wide in (wide2, wide3)]
            nc.scalar.copy(
                out=grouped[0].rearrange("p (t m j) -> p m j t", t=2, j=PACK), in_=src[:, :, :, 0:2]
            )
            (nc.scalar.copy if z == 0 else nc.vector.tensor_copy)(
                out=grouped[1].rearrange("p (t m j) -> p m j t", t=2, j=PACK), in_=src[:, :, :, 2:4]
            )
            for u in range(2):
                w1c[z][u] = sb("w1c%d_%d" % (z, u), [P, 2 * P], U32)
                w1s[z][u] = sb("w1s%d_%d" % (z, u), [P, 2 * P], U8)
                nc.vector.quantize_mx(out=w1c[z][u][:].bitcast(FP8X4), scales=w1s[z][u][:], in_=grouped[u])

        xg = [sb("xg%d" % z, [P, S], U32) for z in range(PASSES)]
        nc.vector.tensor_copy(out=xg[0][:], in_=xw[0][:].indirect(offs_t[:]))
        for lo, hi in ((0, 128), (128, 384), (384, 512)):
            nc.vector.tensor_copy(out=xg[1][:, lo:hi], in_=xw[1][:].indirect(entries(offs_t, lo, hi)))

        emb_v = emb.rearrange("(p t) r -> p t r", t=PACK)
        plain = U - TURNED
        tails = sb("tails", [P, PACK, TURNED], F32, "w1_raw0")
        nc.sync.dma_start(out=tails[:], in_=emb_v[:, :, plain:U])
        emb_low = sb("emb_low", [P, 2, plain], F32, "w1_raw1")
        nc.sync.dma_start(out=emb_low[:], in_=emb_v[:, 0:2, 0:plain])
        nc.sync.dma_start(out=wide2[:, U : U + plain], in_=emb_v[:, 3, 0:plain])
        nc.sync.dma_start(out=wide3[:, U : U + plain], in_=emb_v[:, 2, 0:plain])

        def first_product(acc, z, t, lo, hi):
            u, e = divmod(t, 2)
            nc.tensor.matmul_mx(
                out=acc[:, 0 : hi - lo],
                lhsT=w1c[z][u][:, e * P : (e + 1) * P].bitcast(FP8X4),
                lhsT_scale=w1s[z][u][:, e * P : (e + 1) * P],
                rhs=xg[z][:, lo:hi].bitcast(FP8X4),
                rhs_scale=xs_at[:, z * S + lo : z * S + hi],
                start=(z == 0),
                stop=(z == PASSES - 1),
            )

        def rectify(acc, t, lo, hi, on_scalar, h=None):
            if h is None:
                h = sb("h%d_%d" % (t, lo), [P, hi - lo], F32)[:]
            if on_scalar:
                nc.scalar.activation(out=h, in_=acc[:, 0 : hi - lo], func=RELU)
            else:
                nc.vector.tensor_scalar_max(out=h, in0=acc[:, 0 : hi - lo], scalar1=0.0)
            return h

        def place(t, h, lo, hi):
            target = up[t][:].indirect(entries(cell_t, lo, hi))
            if t % 2:
                nc.scalar.activation(out=target, in_=h, func=COPY)
            else:
                nc.vector.tensor_copy(out=target, in_=h)

        def produce(b, t, lo, hi, on_scalar, h=None):
            acc = bank(b)
            for z in range(PASSES):
                first_product(acc, z, t, lo, hi)
            return rectify(acc, t, lo, hi, on_scalar, h)

        firsts = [bank(0), bank(1)]
        for z in range(PASSES):
            for t in (1, 0):
                first_product(firsts[t], z, t, 0, 128)
        h10 = rectify(firsts[1], 1, 0, 128, True)
        h00 = rectify(firsts[0], 0, 0, 128, True)
        place(1, h10, 0, 128)
        place(0, h00, 0, 128)
        h11 = produce(2, 1, 128, 384, False)
        h01 = produce(3, 0, 128, 384, True)
        place(1, h11, 128, 384)
        place(0, h01, 128, 384)
        h12 = produce(4, 1, 384, 512, False)
        h02 = produce(5, 0, 384, 512, True)
        pairs = sb("pairs", [P, 2 * plain], F32)
        h30 = produce(6, 3, 0, 256, False, pairs[:, plain - SHARE : plain - SHARE + 256])
        place(1, h12, 384, 512)
        place(0, h02, 384, 512)
        h2 = produce(7, 2, 0, 512, True)
        h31 = produce(0, 3, 256, 512, False)
        sums = [bank(6), bank(7)]

        def turn(t, source, opens=False, closes=False):
            nc.tensor.matmul(
                out=sums[t // 2][:, t % 2 * P : (t % 2 + 1) * P],
                lhsT=source,
                rhs=ident[:],
                is_transpose=True,
                start=opens,
                stop=closes,
            )

        for t in range(PACK):
            turn(t, tails[:, t, :], opens=(t % 2 == 0))
        place(3, h30, 0, 256)
        place(2, h2, 0, 512)
        place(3, h31, 256, 512)

        embs = [emb_low[:, 0, :], emb_low[:, 1, :]]
        w2w = sb("w2w", [P, N], U32, "xg0")
        nc.sync.dma_start(out=w2w[:].bitcast(I32), in_=w2_words[0].rearrange("p n t -> p (n t)").bitcast(I32))
        w2s = sb("w2s", [P, N], U8, "w1s0_0")
        nc.gpsimd.memset(w2s[:].bitcast(I32), 0)
        for q in range(4):
            nc.sync.dma_start(
                out=w2s[32 * q : 32 * q + 4, :].bitcast(I32),
                in_=w2_scales[0, 4 * q : 4 * q + 4, :].bitcast(I32),
            )
        gate_t = sb("gate_t", [P, 2, V], F32, "w1c0_1")
        nc.sync.dma_start(out=gate_t[:], in_=gate.rearrange("d p v -> p d v"))

        def words(u, lo, hi):
            return pairs[:, u * plain + lo : u * plain + hi]

        def add_low(engine, t, lo, hi):
            half = words(0, lo, hi).bitcast(BF16).rearrange("p (r e) -> p r e", e=2)[:, :, t]
            engine.tensor_tensor(out=half, in0=up[t][:, lo:hi], in1=embs[t][:, lo:hi], op=ADD)

        def add_high(lo, hi):
            a = wide2[:].rearrange("p (e r) -> p r e", e=2)[:, lo:hi]
            b = wide3[:].rearrange("p (e r) -> p r e", e=2)[:, lo:hi, ::-1]
            both = words(1, lo, hi).bitcast(BF16).rearrange("p (r e) -> p r e", e=2)
            nc.vector.tensor_tensor(out=both, in0=a, in1=b, op=ADD)

        for t in (1, 0):
            add_low(nc.gpsimd, t, 0, plain - SHARE)
        for t in (1, 0):
            add_low(nc.vector, t, plain - SHARE, plain)

        turn(1, up[1][:, plain:U])
        turn(0, up[0][:, plain:U], closes=True)
        turned = sb("turned", [P, 2 * P], F32, "h3_256")

        def round_half(u, copy):
            copy(
                out=turned[:, u * P : (u + 1) * P].bitcast(BF16).rearrange("c (p e) -> c p e", e=2),
                in_=sums[u][:, 0 : 2 * P].rearrange("c (e p) -> c p e", e=2),
            )

        round_half(0, nc.scalar.copy)
        turn(2, up[2][:, plain:U])
        turn(3, up[3][:, plain:U], closes=True)
        round_half(1, nc.scalar.copy)
        back = bank(7)
        for u in range(2):
            nc.tensor.transpose(back[:, u * P : (u + 1) * P], turned[:, u * P : (u + 1) * P], ident[:])

        edges = (0, 256, 512, 768, 896, 1024)
        chunks = list(zip(edges, edges[1:]))
        zq = [sb("zi%d" % c, [P, (hi - lo) * PACK], BF16)[:] for c, (lo, hi) in enumerate(chunks[:3])]

        def weave(c, copy):
            lo, hi = chunks[c]
            copy(
                out=zq[c].bitcast(F32).rearrange("p (r i u) -> p r u i", u=2, i=2),
                in_=pairs[:].rearrange("p (u r i) -> p r u i", u=2, i=2)[:, lo // 2 : hi // 2],
            )

        y = sb("y", [P, U], F32, "wide2")

        def second_product(c, acc):
            lo, hi = chunks[c]
            zc = sb("zc%d" % c, [P, hi - lo], U32, "pairs" if c == 3 else None)
            zs = sb("zs%d" % c, [P, hi - lo], U8)
            nc.vector.quantize_mx(out=zc[:].bitcast(FP8X4), scales=zs[:], in_=zq[c])
            nc.tensor.matmul_mx(
                out=acc,
                lhsT=w2w[:].bitcast(FP8X4),
                lhsT_scale=w2s[:],
                rhs=zc[:].bitcast(FP8X4),
                rhs_scale=zs[:],
                start=True,
                stop=True,
            )

        accs = [bank(b) for b in (1, 2, 3, 4, 5)]
        for c in (0, 1, 2):
            add_high(*chunks[c])
        add_high(*chunks[3])
        for c in (0, 1, 2):
            weave(c, nc.scalar.copy)
        second_product(0, accs[0][:, 0:256])
        last = sb("last", [P, 2 * TURNED * PACK], BF16, "wide3")
        zq.extend([last[:, 0 : TURNED * PACK], last[:, TURNED * PACK :]])
        weave(3, nc.scalar.copy)
        nc.vector.tensor_copy(
            out=zq[4].bitcast(F32).rearrange("p (r u) -> p r u", u=2),
            in_=back[:, 0 : 2 * P].rearrange("p (u r) -> p r u", u=2),
        )
        for c in range(1, len(chunks)):
            second_product(c, accs[c][:, 0 : chunks[c][1] - chunks[c][0]])
        for c, (lo, hi) in enumerate(chunks):
            (nc.vector.tensor_copy if c == 3 else nc.scalar.copy)(out=y[:, lo:hi], in_=accs[c][:, 0 : hi - lo])

        parts = [(0, 256), (256, 512)]
        first = [sb("first%d" % a, [P, hi - lo], F32) for a, (lo, hi) in enumerate(parts)]
        second = [sb("second%d" % a, [P, hi - lo], F32) for a, (lo, hi) in enumerate(parts)]
        for a, (lo, hi) in enumerate(parts):
            nc.scalar.activation(out=second[a][:], in_=y[:].indirect(entries(pos_t[1], lo, hi)), func=COPY)
            nc.vector.tensor_tensor(
                out=first[a][:], in0=y[:].indirect(entries(pos_t[0], lo, hi)), in1=gate_t[:, 0, lo:hi], op=MULT
            )
        weighted = [sb("weighted%d" % a, [P, hi - lo], F32) for a, (lo, hi) in enumerate(parts)]
        for a, (lo, hi) in enumerate(parts):
            nc.vector.tensor_tensor(out=weighted[a][:], in0=second[a][:], in1=gate_t[:, 1, lo:hi], op=MULT)
        for a, (lo, hi) in enumerate(parts):
            o = sb("o%d" % a, [P, hi - lo], F32)
            nc.vector.tensor_tensor(out=o[:], in0=first[a][:], in1=weighted[a][:], op=ADD)
            nc.sync.dma_start(out=out[:, lo:hi], in_=o[:])
